import numpy as np, ml_dtypes
CORES = [242,247,114,119]
N = 4
BF = ml_dtypes.bfloat16
W, V, L, S, T, E = 2048, 512, 128, 16, 5, 1
def parts(rng):
    x = (64 * rng.random((N, 8, 16, W)) * (0.5 + 0.5 * rng.random((N, 8, 1, W)))).astype(np.int64)
    im = (64 * rng.random((N, 8, 16, V)) * (0.25 + 0.75 * rng.random((N, 8, 1, V)))).astype(np.int64)
    z = (64 * rng.random((N, 8, 16, 2, L)) * (0.5 + 0.5 * rng.random((N, 8, 1, 2, L)))).astype(np.int64)
    b = rng.integers(0, W, (N, 8, 16, V)); q = np.minimum((8 * rng.random((N, 8, 16, V)) ** 0.6).astype(np.int64), 7)
    return x, im, b, q, z, rng.integers(1, 4096, (N, 8, 16))
def pack(x, im, b, q, z, w):
    return {"geno": x.reshape(N, 128, W).astype(np.float32).astype(BF), "immun": im.reshape(N, 128, V).astype(np.float32).astype(BF),
            "bank": (b + W * q).reshape(N, 128, V).astype(np.int32), "bites": z.reshape(N, 128, 2 * L).astype(np.float32).astype(BF), "wt": w.reshape(N, 128, 1).astype(np.int32)}
def first(z, w):
    u = np.sum(w[:, :, :, None] * z[:, :, :, 0], axis=2) & 4095
    return ((u * u >> 5) + 37 * u) & (V - 1)
def setup_inputs(rng):
    return pack(*parts(rng))
def setup_inputs_corners(rng):
    x, im, b, q, z, w = parts(rng); w[:, :, 0] = 4095; w[:, :, 1] = 2048
    kind = rng.integers(0, 4, (N, 8, 1, V)); im = np.where(kind == 0, 0, np.where(kind == 1, 63, im))
    mode = rng.integers(0, 7, (N, 8, 1, V)); pos = np.argsort(rng.random((N, 8, 16, V)), axis=2); near = E - 1 + rng.integers(0, 3, q.shape)
    q = np.where(mode == 5, q[:, :, :1], q); q = np.where(mode == 4, near, q); q = np.where(mode == 3, 7 * (pos < 2), q)
    q = np.where(mode == 2, 7 * (pos < 1), q); q = np.where(mode == 1, 0, q); q = np.where(mode == 0, 7, q)
    edge = rng.integers(0, 4, (N, 8, 1, V)); b = np.where(edge == 0, (W - 1) * rng.integers(0, 2, b.shape), b); b = np.where(edge == 1, b[:, :, :1], b)
    z[:, :, :, 0, 4:L - 1] = np.maximum(z[:, :, :, 0, 4:L - 1], 1)
    z[:, :, :, :, 0] = 0; z[:, :, :, :, 1] = 63; z[:, :, :, :, 2] = 0; z[:, :, 1, :, 2] = 1; z[:, :, :, :, L - 1] = 0; z[:, :, 0, :, L - 1] = 1
    v = first(z, w); n = L // 2; m = L // 8
    for a in range(N):
        for g in range(8):
            lanes = (4 + rng.permutation(L - 5))[:n]; zz = z[a, g, :, 0][:, lanes]
            po = np.argsort(rng.random((16, n)), axis=0); cnt = 8 + np.arange(n) % 3
            im[a, g][:, v[a, g, lanes]] = zz - (po < cnt)
            own = lanes[:m]; k = rng.integers(0, 16, m); h = v[a, g, own]
            b[a, g, k, h] = S * own; q[a, g, k, h] = 7
            x[a, g][:, S * own] = np.where(zz[:, :m] < 32, 63, 0)
    return pack(x, im, b, q, z, w)
def setup_inputs_crowd(rng):
    x, im, b, q, z, w = parts(rng); w = np.repeat(rng.integers(1, 4096, (N, 8, 1)), 16, axis=2)
    for a in range(N):
        for g in range(8):
            for c in range(2):
                n = int(rng.choice(np.array([1, 2, 5, 17, 30])))
                if g == a % 8 and c == 0: n = 1
                if g == (a + 3) % 8 and c == 0: continue
                base = z[a, g, :, c, :n].copy()[:, rng.integers(0, n, L)]
                z[a, g, :, c] = np.take_along_axis(base, np.argsort(rng.random((16, L)), axis=0), 0)
        g = (a + 3) % 8; w[a, g] = rng.integers(1, 4096, 16); w[a, g, 0] = 1; w[a, g, 15] = 64
        u = rng.permutation(4096); u = u[np.unique(((u * u >> 5) + 37 * u) & (V - 1), return_index=True)[1]]
        need = (rng.permutation(u)[:L] - np.sum(w[a, g, 1:15, None] * z[a, g, 1:15, 0], axis=0)) & 4095
        z[a, g, 0, 0] = need & 63; z[a, g, 15, 0] = need >> 6
    return pack(x, im, b, q, z, w)
def setup_inputs_ends(rng):
    def rec(n):
        k = rng.integers(0, 3, (N, 8, 1, n)); return 63 * np.where(k == 2, rng.integers(0, 2, (N, 8, 16, n)), k)
    x = rec(W); im = rec(V); z = rec(2 * L).reshape(N, 8, 16, 2, L); w = np.where(rng.integers(0, 2, (N, 8, 16)) == 1, 4095, 1); w[N - 1, 7] = 4095
    x[:, 1::2, :, W - 1] = 0; x[:, ::2, :, W - 1] = 63 * rng.integers(0, 2, (N, 4, 16))
    nz = rng.integers(0, 8, (8, 1, L)) * rng.integers(0, 2, (8, 1, L)); nz[:, :, 0] = 0; nz[:, :, L - 1] = 0
    nz[0, 0, ::2] = 0; nz[0, 0, 1] = 1; nz[0, 0, L - 1] = 0
    z[N - 1, :, :, 0] = 63 * (np.argsort(rng.random((8, 16, L)), axis=1) >= nz)
    z[1, :, :, 0] = 63 * (np.argsort(rng.random((8, 16, L)), axis=1) >= rng.integers(0, 8, (8, 1, L)))
    v = first(z, w); r = np.arange(16)[None, None, :, None]; mode = rng.integers(0, 5, (N, 8, 1, V))
    fl = (mode == 0) | ((mode == 1) & (r >= 14)) | ((mode == 2) & ((r == 0) | (r == 15))) | ((mode == 4) & (rng.random((N, 8, 16, V)) < 0.5))
    anyb = (rng.random((N, 8, 1, V)) < 0.5) & fl
    for g in range(8):
        for a in (1, N - 1):
            h = v[a, g]; fl[a, g, 14:][:, h] = True; anyb[a, g][:, h] = False; im[a, g][:, h] = 0
        im[0, g][:, v[0, g]] = 63
    im[N - 1, 0][:, v[N - 1, 0, 1]] = 63
    woke = 16 * L - 2 * int(np.sum(v[N - 1, 0] == v[N - 1, 0, 1])); assert woke > 15 * L and woke & (V - 1) != 0
    b = np.where(fl, np.where(anyb, rng.integers(0, W, fl.shape), W - 1), 0); q = 7 * fl
    for g, ks in ((1, (2, 5, 9)), (3, (0, 1, 15)), (5, (13, 14, 15))):
        h = v[N - 1, g, 0]; x[N - 1, g, :, W - 2] = 0; x[N - 1, g, rng.integers(0, 16), W - 2] = 1
        b[N - 1, g, :, h] = 0; q[N - 1, g, :, h] = 0
        for k, c in zip(ks, (W - 2, W - 2, W - 1)):
            b[N - 1, g, k, h] = c; q[N - 1, g, k, h] = 7
    return pack(x, im, b, q, z, w)
def setup_inputs_spread(rng):
    x, im, b, q, z, w = parts(rng)
    def pw(*s): return rng.random(s) ** np.exp2(rng.integers(-2, 4, s[:2] + (1,) + s[3:]))
    x = np.minimum((64 * pw(N, 8, 16, W)).astype(np.int64), 63); im = np.minimum((64 * pw(N, 8, 16, V)).astype(np.int64), 63)
    z = np.minimum((64 * pw(N, 8, 16, 2, L)).astype(np.int64), 63); b = np.minimum((W * pw(N, 8, 16, V)).astype(np.int64), W - 1)
    q = np.minimum((8 * rng.random((N, 8, 16, V)) ** np.exp2(rng.integers(-2, 2, (N, 8, 1, V)))).astype(np.int64), 7)
    w = np.minimum(np.exp2(12 * rng.random((N, 8, 16))).astype(np.int64), 4095)
    return pack(x, im, b, q, z, np.maximum(w, 1))
def setup_inputs_ties(rng):
    lv = rng.integers(0, 3, (N, 8, 1, W)); x = lv + rng.integers(0, 3, (N, 8, 16, W)); im = rng.integers(0, 3, (N, 8, 16, V))
    z = rng.integers(0, 3, (N, 8, 1, 2, L)) + rng.integers(0, 3, (N, 8, 16, 2, L)); w = rng.integers(1, 4096, (N, 8, 16)); b = rng.integers(0, W, (N, 8, 16, V))
    q = np.where(rng.random((N, 8, 16, V)) < 0.5, rng.integers(0, 8, (N, 8, 1, V)), rng.integers(4, 8, (N, 8, 1, V)))
    x[:, ::2, :, W // 2:] = x[:, ::2, :, :W // 2]; b[:, :, 8:, ::2] = b[:, :, :8, ::2]
    z[:, :, :, 0, ::4] = np.take_along_axis(x, rng.integers(0, W, (N, 8, 1, L // 4)), 3)
    x[:, 1::2] += 59; im[:, 1::2] += 59; z[:, 1::2] += 59
    r = np.arange(16)[:, None]; x[:, 2] = (r + np.arange(W)) % 3; z[:, 2, :, 0] = (r + np.arange(L)) % 3; im[:, 2] = 0
    same = ((4, 0, [15]), (6, L // 2, [2, 15]), (7, L - 1, [15])); cz = rng.integers(0, W, (N, 8))
    for a in range(N):
        for g, j, ks in same:
            e = 59 * (g % 2) + rng.integers(1, 3, 16); z[a, g, :, 0, j] = e; x[a, g, :, cz[a, g]] = e
    v = first(z, w)
    for a in range(N):
        for j in range(3):
            h = v[a, 2, j]; q[a, 2, :, h] = 0; q[a, 2, 3, h] = 7; q[a, 2, 12, h] = 7
            b[a, 2, 3, h] = 3 * rng.integers(0, W // 3) + (j + 1) % 3; b[a, 2, 12, h] = 3 * rng.integers(0, W // 3) + (j + 2) % 3
        for g, j, ks in same:
            h = v[a, g, j]; im[a, g, :, h] = 0; q[a, g, :, h] = 0; b[a, g, 15, h] = cz[a, g]
            for k in ks: q[a, g, k, h] = 7
    return pack(x, im, b, q, z, w)
def check_inputs(d):
    bad = []
    for k, lo, hi in (("geno", 0, 63), ("immun", 0, 63), ("bank", 0, 8 * W - 1), ("bites", 0, 63), ("wt", 1, 4095)):
        a = np.asarray(d[k]).astype(np.float64)
        if not np.all((a >= lo) & (a <= hi)): bad.append("range of " + k)
        elif np.any(a != np.floor(a)): bad.append("whole numbers of " + k)
    return bad
def beats(a, c):
    return (np.sum(a > c, axis=2) >= 9).astype(np.int64)
def reference(geno, immun, bank, bites, wt):
    X = geno.astype(np.float32).astype(np.int64).reshape(N, 8, 16, W); im = immun.astype(np.float32).astype(np.int64).reshape(N, 8, 16, V)
    bk = bank.astype(np.int64).reshape(N, 8, 16, V); z = bites.astype(np.float32).astype(np.int64).reshape(N, 8, 16, 2, L); w = wt.astype(np.int64).reshape(N, 8, 16, 1)
    todo = [z[:, :, :, 0], np.roll(z[:, :, :, 1], 1, axis=0)]
    A = np.zeros(N, np.int64); row = np.arange(16)[None, None, :, None]; lane = np.arange(L)[None, None, None, :]
    for t in range(T):
        s = todo[t]
        u = np.sum(w * s, axis=2) & 4095; v = ((u * u >> 5) + 37 * u + A[:, None, None]) & (V - 1)
        e = np.take_along_axis(bk, v[:, :, None, :], 3); b = e & (W - 1); q = e // W
        iv = np.take_along_axis(im, v[:, :, None, :], 3)
        c = np.take_along_axis(X, b.reshape(N, 8, 1, 16 * L), 3).reshape(N, 8, 16, 16, L)
        D = np.sum(np.abs(c - s[:, :, :, None, :]), axis=2)
        sick = np.sum(s > iv, axis=2) >= 9
        key = np.where((q >= t + E) & sick[:, :, None, :], D * 16 + 15 - row, -1)
        k1 = np.argmax(key, axis=2); h1 = (np.max(key, axis=2) >= 0).astype(np.int64)
        key = np.where(row == k1[:, :, None, :], -1, key)
        k2 = np.argmax(key, axis=2); h2 = (np.max(key, axis=2) >= 0).astype(np.int64)
        a1 = np.take_along_axis(c, k1[:, :, None, None, :], 3)[:, :, :, 0]; a2 = np.take_along_axis(c, k2[:, :, None, None, :], 3)[:, :, :, 0]
        n0 = h1 * beats(a1, s) + h2 * beats(a2, s); n1 = beats(s, a1) + h2 * beats(a2, a1); n2 = beats(s, a2) + beats(a1, a2)
        o = np.argsort(np.stack([n0 * 4, np.where(h1 == 1, n1 * 4 + 1, 97), np.where(h2 == 1, n2 * 4 + 2, 98)]), axis=0)
        st = np.stack([s, a1, a2]); second = np.where(h1 == 1, o[1], 0)
        f = np.take_along_axis(st, o[0][None, :, :, None, :], 0)[0]; m = np.take_along_axis(st, second[None, :, :, None, :], 0)[0]
        todo.append(np.roll(np.where((u[:, :, None, :] >> (row & 7)) & 1 == 1, f, m), 2, axis=0))
        wake = ((row == k1[:, :, None, :]) & (h1[:, :, None, :] == 1)) | ((row == k2[:, :, None, :]) & (h2[:, :, None, :] == 1))
        q = np.where(wake, 0, q); slot = np.argmin(q * 16 + row, axis=2)
        e = np.where(row == slot[:, :, None, :], S * lane + t + W * (8 + t), b + W * q); iv = np.maximum(iv - 1, f)
        for a in range(N):
            for g in range(8):
                hv, fi = np.unique(v[a, g], return_index=True)
                bk[a, g][:, hv] = e[a, g][:, fi]; im[a, g][:, hv] = iv[a, g][:, fi]
        X[:, :, :, t::S] = s
        A = np.sum(h1 + h2, axis=(1, 2))
    return {"ybank": bk.reshape(N, 128, V).astype(np.float32), "yimm": im.reshape(N, 128, V).astype(np.float32).astype(BF), "ygeno": X.reshape(N, 128, W).astype(np.float32).astype(BF)}

@@ -1,0 +1,573 @@
+from concourse.mybir import AluOpType as O, AxisListType, ActivationFunctionType as AF
+
+BF, F4, I4, U2 = "bfloat16", "float32", "int32", "uint16"
+SIZE = {BF: 2, U2: 2, F4: 4, I4: 4}
+ONE = {
+    "gz": (2688, BF), "zb1": (128, BF), "bki": (512, I4), "bt0": (512, I4), "btab": (640, F4), "qtab": (640, BF), "itab": (640, BF),
+    "wti": (1, I4), "wlo": (1, I4), "whi": (1, I4), "wlof": (1, F4), "whif": (1, F4),
+    "m16": (256, F4), "ident": (128, BF), "idf": (128, F4), "nid": (128, BF), "tri": (128, BF), "tz": (128, BF), "blk": (128, BF),
+    "blk0": (128, BF), "hot": (128, BF), "pi": (1, I4), "bd": (8, BF), "rf0": (8, F4), "rf": (8, F4), "rb": (8, BF), "r1k": (8, BF),
+    "lr": (2048, BF), "whb": (128, BF), "wlb": (128, BF), "rs": (128, F4), "bcf": (16, F4), "bco": (16, U2), "onb": (128, BF),
+    "onf": (128, F4), "onn": (128, F4), "c6k": (128, BF), "c23": (16, BF), "crow": (128, BF), "lrow": (128, BF), "rrow": (128, BF), "qrow": (8, BF),
+    "oht": (2304, BF), "zt": (2320, BF), "iv": (256, I4), "c2": (1, F4), "c8": (1, F4), "qr": (512, F4), "qm": (512, F4), "ft": (512, BF), "ubt": (256, BF), "uv2": (256, I4), "uv2b": (256, I4), "pw": (16, F4),
+    "half": (16, F4), "zero": (16, F4), "li": (8, I4), "trc": (8, I4), "kc": (16, F4),
+    "newr": (640, F4), "irow": (128, F4), "chalf": (128, BF), "ctwo": (128, BF), "wrow": (128, BF),
+    "vrow": (128, BF), "wm": (16, BF), "m16w": (128, F4), "k3l": (128, BF), "k3r": (128, BF), "bigi": (128, BF), "i16": (128, BF),
+    "cr0": (128, BF), "cr1": (128, BF), "cr2": (128, BF), "yb": (512, F4), "q2": (512, F4),
+}
+for _i in range(8):
+    ONE["a%d" % _i] = (1, I4)
+    ONE["b%d" % _i] = (1, F4)
+    ONE["h%d" % _i] = (16, F4)
+TWO = {
+    "um": (128, F4), "us": (128, F4), "ui": (8, I4), "ua": (8, I4), "u8": (8, I4), "xq": (8, F4), "sq": (8, I4), "bs": (8, I4),
+    "ul": (8, U2), "bl": (8, U2), "fe": (128, BF), "fo": (128, BF), "e1": (1024, BF), "dl": (128, BF), "du": (8, F4), "dtr": (8, I4),
+    "zx": (2048, BF), "x": (2320, BF), "ab": (2048, BF), "bo": (128, U2), "bg": (128, F4), "qg": (128, BF),
+    "ig": (128, BF), "ub": (128, BF), "vt": (8, I4), "vi": (8, I4), "vl": (8, U2), "oi": (8, I4), "ol": (8, U2),
+    "ss": (256, F4), "y": (128, F4), "sg": (16, F4), "ac": (1, F4), "L": (256, F4), "sw": (128, F4), "gL": (128, BF), "mi": (16, I4),
+    "Z": (16, I4), "Zm": (8, I4), "G": (8, I4), "gl": (8, U2), "oh": (128, BF), "za": (256, BF), "oq": (128, BF),
+    "bn": (128, F4), "qn": (128, BF), "inn": (128, BF), "im1": (128, BF), "xl": (16, U2),
+    "pz": (8, BF), "oK": (16, F4), "gs": (128, BF), "pen": (128, BF), "pq": (128, BF), "X": (384, BF), "cm": (768, BF),
+    "bb": (48, BF), "K": (24, F4), "mm": (24, F4), "fm": (16, I4), "fa": (16, I4), "fl": (16, U2), "xf": (256, BF),
+    "db": (128, BF),
+}
+_OWN = ("gz", "zb1", "bki", "btab", "qtab", "itab", "wti", "yb", "cr0", "cr1", "cr2", "x", "zx", "ab", "oht", "zt", "k3l", "k3r")
+SCRATCH, PLACE, STRIDE, _fill = {}, {}, {}, {BF: 0, F4: 0, I4: 0, U2: 0}
+for _t, _m in ((ONE, 1), (TWO, 2)):
+    for _k, (_n, _d) in _t.items():
+        STRIDE[_k] = -(-_n // 16) * 16
+        if _k in _OWN:
+            SCRATCH[_k] = ("sbuf", [128, STRIDE[_k] * _m if _m == 2 else _n], _d)
+            PLACE[_k] = (_k, 0)
+        else:
+            PLACE[_k] = ("all_" + _d, _fill[_d])
+            _fill[_d] += STRIDE[_k] * _m
+for _d, _n in _fill.items():
+    SCRATCH["all_" + _d] = ("sbuf", [128, _n], _d)
+PS = ("pk", "pu", "p1", "p2", "p3", "p4", "p5", "p6")
+for _k in PS:
+    SCRATCH[_k] = ("psum", [128, 512], F4)
+    PLACE[_k] = (_k, 0)
+SEMAPHORES = ["c%d" % _i for _i in range(100)] + ["d%d" % _i for _i in range(40)] + ["rz1", "rz2", "rz3", "rz4", "snd"]
+NET = [5.0, 3.0]
+GK, VK = 8, 8
+BONUS = {"cross": 2.0, "imm": 8.0, "sick": 2.0, "host0": 2.0, "dup1": -4.0, "top": -4.0, "u1": -2.0}
+WAKE = 0.09
+
+
+def rank_program(g, core, T, topo):
+    rank = T.rank_of(core)
+    if rank is None:
+        return
+    N = len(T.cores)
+    eng = {"v": g.vector, "s": g.scalar, "t": g.tensor, "g": g, "y": g.sync}
+    ops = []
+    step = [0]
+    tag = ["set"]
+
+    def R(n, a, b, st=1, p0=0, p1=128, off=None):
+        if n in TWO:
+            a, b = a + (step[0] & 1) * STRIDE[n], b + (step[0] & 1) * STRIDE[n]
+        return (n, a, b, st, p0, p1, off)
+
+    def f(n, off=None):
+        return R(n, 0, (TWO[n] if n in TWO else ONE[n])[0], off=off)
+
+    def ap(r):
+        n, a, b, st, p0, p1, off = r
+        n, c = PLACE[n]
+        x = T[n][p0:p1, c + a:c + b] if st == 1 else T[n][p0:p1, c + a:c + b:st]
+        return x.indirect(ap(off)) if off else x
+
+    def wide(r):
+        return 16 * (r[6][2] - r[6][1]) if r[6] else -(-(r[2] - r[1]) // r[3])
+
+    def small(*rs):
+        return all(r[0] not in PS and (TWO[r[0]] if r[0] in TWO else ONE[r[0]])[1] in (BF, U2) for r in rs)
+
+    def run(q, calls, reads, writes, cost, **kw):
+        regs = [(r, 0) for r in reads] + [(r, 1) for r in writes] + [(r[6], 0) for r in list(reads) + list(writes) if r[6]]
+        ops.append(dict(q=q, calls=calls, regs=regs, cost=cost, tag=tag[0], **kw))
+        return len(ops) - 1
+
+    def vcost(n, o, ins):
+        if o[6]:
+            return 0.05 + 3.5 * wide(o) * 0.00083
+        if any(isinstance(a, tuple) and a[6] for a in ins):
+            return 0.05 + 1.5 * wide(o) * 0.00083
+        return 0.02 + max(64, n) * 0.001
+
+    def tt(o, a, b, op):
+        n = wide(o) * (1 if a[0] in PS or b[0] in PS else 2)
+        run("v", [lambda e: e.tensor_tensor(ap(o), ap(a), ap(b), op)], [a, b], [o], vcost(n, o, [a]))
+
+    def ts(o, a, s1, op0, s2=None, op1=None):
+        rd = [a] + [s for s in (s1, s2) if isinstance(s, tuple)]
+        val = lambda s: ap(s) if isinstance(s, tuple) else s
+        c = vcost(wide(o) * (0.5 if small(o, a) else 1), o, [a])
+        if op1 is None:
+            run("v", [lambda e: e.tensor_scalar(ap(o), ap(a), val(s1), None, op0)], rd, [o], c)
+        else:
+            run("v", [lambda e: e.tensor_scalar(ap(o), ap(a), val(s1), val(s2), op0, op1)], rd, [o], c)
+
+    def cp(o, a):
+        run("v", [lambda e: e.tensor_copy(ap(o), ap(a))], [a], [o], vcost(wide(o) * (0.5 if small(o, a) else 1), o, [a]))
+
+    def scan(o, a, b, op0, op1, init=0.0):
+        run("v", [lambda e: e.tensor_tensor_scan(ap(o), ap(a), ap(b), init, op0, op1)], [a, b], [o], vcost(wide(o), o, []))
+
+    def red(o, a):
+        run("v", [lambda e: e.tensor_reduce(ap(o), ap(a), AxisListType.X, O.add)], [a], [o], vcost(wide(a), o, []))
+
+    def ms(o, c):
+        run("v", [lambda e: e.memset(ap(o), c)], [], [o], vcost(wide(o) * (0.5 if small(o) else 1), o, []))
+
+    def act(o, a, fn=AF.Copy, bias=None, scale=None, accum=None):
+        kw = {}
+        for nm, val in (("bias", bias), ("scale", scale), ("accum_out", accum)):
+            if val is not None:
+                kw[nm] = val
+
+        def call(e):
+            return e.activation(ap(o), ap(a), fn, **{m: ap(v) if isinstance(v, tuple) else v for m, v in kw.items()})
+        run("s", [call], [a] + [v for v in (bias, scale) if isinstance(v, tuple)], [o] + ([accum] if accum else []), vcost(wide(o), o, [a]) + 0.01)
+
+    def mm(lst, grp=None):
+        c = 0.02
+        for z in lst:
+            m = wide(z[1])
+            c += max(min(64, m), wide(z[2])) * 0.001 * (1 if small(z[1]) else 4)
+        run("t", [lambda e, z=z: e.matmul(ap(z[0]), ap(z[1]), ap(z[2]), z[3], z[4]) for z in lst],
+            [z[1] for z in lst] + [z[2] for z in lst], [z[0] for z in lst], c, grp=grp)
+
+    def iota(o, pat, base, cm, whole=True):
+        kw = {} if whole else {"allow_small_or_imprecise_dtypes": True}
+        run("g", [lambda e: e.iota(ap(o), pat, base, cm, **kw)], [], [o], 0.13 + 0.002 * wide(o))
+
+    def keep(o, a, pat, cmp, fill, base, cm):
+        run("g", [lambda e: e.affine_select(ap(o), ap(a), pat, cmp, fill, base, cm)], [a], [o], 0.17 + 0.002 * wide(o))
+
+    def load(q, o, src):
+        run(q, [lambda e: e.dma_start(ap(o), src)], [], [o], 2.0 + (wide(o) * SIZE[ONE[o[0]][1]] * 128) / 200e3, dma=True)
+
+    def store(q, dst, a):
+        run(q, [lambda e: e.dma_start(dst, ap(a))], [a], [], 2.0, dma=True)
+
+    sent, lands = [0], []
+
+    def send(dst, t, a):
+        o, rsem = R("gz", 2048 + 128 * t, 2176 + 128 * t), "rz%d" % t
+        rid, pid = topo.addr(dst, core)
+        m, ne = 0, 0
+        for e in topo.engines(core, dst)[:8]:
+            m, ne = m | 1 << e, ne + 1
+        sent[0] += ne
+        k = run("g", [lambda e: e.remote_dma(ap(o), ap(a), T.sem[rsem], T.sem["snd"], pid, rid, m)], [a], [], 0.5, sem=("snd", sent[0]))
+        src = T.cores[(2 * rank - T.rank_of(dst)) % N]
+        n = len(topo.engines(src, core)[:8])
+        run("net", [], [], [o], NET[0] if lands else NET[0] + NET[1], sem=(rsem, n), after=k)
+        lands.append((rsem, n))
+
+    def zb(t):
+        return R("gz", 2048 + 128 * t, 2176 + 128 * t)
+
+    load("y", f("wti"), T.wt[:])
+    load("s", zb(0), T.bites[:, 0:128])
+    load("s", f("zb1"), T.bites[:, 128:256])
+    load("y", f("bki"), T.bank[:])
+    load("y", R("gz", 0, 1024), T.geno[:, 0:1024])
+    load("s", R("gz", 1024, 2048), T.geno[:, 1024:2048])
+    load("y", R("itab", 0, 512), T.immun[:])
+    send(T.cores[(rank + 1) % N], 1, f("zb1"))
+
+    iota(f("pi"), [[0, 1]], 0, 1)
+    ms(f("onb"), 1.0)
+    ms(f("onf"), 1.0)
+    ms(f("tz"), 0.0)
+    keep(f("hot"), f("onb"), [[0, 8], [-1, 16]], O.is_equal, 0.0, 0, 1)
+    keep(f("blk0"), f("onb"), [[-16, 8], [0, 16]], O.is_ge, 0.0, 0, 1)
+    keep(f("blk"), f("blk0"), [[16, 8], [0, 16]], O.is_ge, 0.0, 15, -1)
+    keep(f("rs"), f("onf"), [[0, 8], [1, 16]], O.is_gt, 0.0, 0, 0)
+    keep(f("rf0"), R("onf", 0, 8), [[-16, 8]], O.is_ge, 0.0, 0, 1)
+    keep(f("rf"), f("rf0"), [[16, 8]], O.is_ge, 0.0, 15, -1)
+    keep(f("ident"), f("onb"), [[-1, 128]], O.is_equal, 0.0, 0, 1)
+    keep(f("idf"), f("onf"), [[-1, 128]], O.is_equal, 0.0, 0, 1)
+    iota(f("bcf"), [[16, 16]], 15, 0, False)
+    iota(f("iv"), [[1, 256]], 0, 0)
+    iota(f("irow"), [[1, 128]], 0, 0, False)
+    iota(f("crow"), [[0, 8], [1, 16]], -256, 0, False)
+    iota(f("lrow"), [[16, 128]], 0, 0, False)
+    iota(f("rrow"), [[0, 8], [16, 16]], 0, 0, False)
+    iota(f("qrow"), [[256, 8]], 256, 0, False)
+    iota(f("li"), [[16, 8]], 512, 0)
+
+    def part(j, op, val):
+        ts(f("a%d" % j), f("pi"), val, op)
+        cp(f("b%d" % j), f("a%d" % j))
+
+    part(2, O.bitwise_and, 15)
+    part(4, O.bitwise_and, 16)
+    ts(f("wlo"), f("wti"), 63, O.bitwise_and)
+    ts(f("whi"), f("wti"), 4032, O.bitwise_and)
+    cp(f("wlof"), f("wlo"))
+    cp(f("whif"), f("whi"))
+    act(f("wlb"), f("blk"), scale=f("wlof"))
+    act(f("whb"), f("blk"), scale=f("whif"))
+    mm([(R("p1", 0, 128), f("hot"), f("hot"), True, True)])
+    for j in (0, 128):
+        act(R("m16", j, j + 128), R("p1", 0, 128))
+        act(R("zt", j, j + 128), R("p1", 0, 128), scale=-16.0)
+        act(R("oht", j, j + 128), R("p1", 0, 128), scale=8192.0, bias=-8192.0)
+    for n, a, w in (("oht", 256, 256), ("zt", 256, 256), ("oht", 512, 256), ("zt", 512, 256), ("oht", 768, 256), ("zt", 768, 256),
+                    ("oht", 2048, 256), ("oht", 1024, 1024), ("zt", 1024, 1024)):
+        run("y", [lambda e, n=n, a=a, w=w: e.dma_start(ap(R(n, a, a + w)), ap(R(n, 0, w)))],
+            [R(n, 0, w)], [R(n, a, a + w)], 2.3, dma=True)
+    ms(R("zt", 2048, 2320), 0.0)
+    act(f("rb"), f("rf"))
+    act(f("bd"), f("rf"), scale=-4096.0)
+    ts(f("bt0"), f("bki"), 2047, O.bitwise_and)
+    ts(R("btab", 0, 512), f("bt0"), 4097.0 / 4096.0, O.mult)
+    ts(f("qr"), f("bki"), -1023.5, O.add, 1.0 / 2048, O.mult)
+    act(f("qm"), f("qr"), AF.Identity, bias=12582912.0)
+    act(R("qtab", 0, 512), f("qm"), AF.Identity, bias=-12582912.0)
+    ms(f("onn"), -1.0)
+    ms(f("c6k"), -6144.0)
+    ms(f("c23"), 2304.0)
+    act(f("bigi"), f("ident"), scale=8388608.0)
+    act(f("i16"), f("ident"), scale=16.0)
+    act(f("nid"), f("ident"), scale=-1.0)
+    cp(f("bco"), f("bcf"))
+    for t in range(5):
+        act(R("newr", 128 * t, 128 * t + 128, 1, 0, 1), R("irow", 0, 128, 1, 0, 1), AF.Copy, scale=1.0 + 16 / 4096.0,
+            bias=2048.0 + 128 * t + t / 4096.0)
+    ms(f("half"), 0.5)
+    ms(f("zero"), 0.0)
+    scan(f("pw"), f("half"), f("zero"), O.mult, O.add, 1024.0)
+    for j in (0, 8):
+        cp(R("h0", j, j + 8), R("pw", 0, 8))
+    tt(f("h1"), R("m16", 0, 16), f("h0"), O.mult)
+    red(f("b6"), f("h1"))
+    ts(f("uv2"), f("iv"), f("b6"), O.mult)
+    ts(f("uv2b"), f("uv2"), 512, O.bitwise_and)
+    ts(f("ubt"), f("uv2b"), 1.0 / 512, O.mult)
+    ts(f("b3"), f("b4"), -1.0 / 16, O.mult, 1.0, O.add)
+    ts(f("b7"), f("b4"), 1.0 / 16, O.mult)
+    red(f("b5"), R("m16", 0, 8))
+    act(f("c2"), f("b5"), scale=2.0)
+    act(f("c8"), R("m16", 8, 9), scale=2.0, bias=-1.0)
+    act(R("ft", 0, 256), f("ubt"), AF.Identity, scale=f("c2"), bias=-1.0)
+    act(R("ft", 256, 512), f("ubt"), AF.Identity, scale=f("c2"), bias=f("c8"))
+    ms(f("chalf"), 0.5)
+    ms(f("ctwo"), 2.0)
+    P0 = lambda n: R(n, 0, 128, 1, 0, 1)
+    scan(P0("wrow"), P0("chalf"), P0("tz"), O.mult, O.add, 2.0 ** 64)
+    scan(P0("vrow"), P0("ctwo"), P0("tz"), O.mult, O.add, 2.0 ** -66)
+    mm([(R("p2", 0, 16), P0("wrow"), R("onb", 0, 16, 1, 0, 1), True, True), (R("p2", 16, 17), P0("vrow"), R("onb", 0, 1, 1, 0, 1), True, True)])
+    act(f("wm"), R("p2", 0, 16))
+    act(f("b1"), R("p2", 16, 17))
+    act(f("m16w"), R("m16", 0, 128), scale=f("b1"))
+    for n, rows in (("k3l", ("onb", "lrow", "onb")), ("k3r", ("crow", "onb", "c6k"))):
+        for j, m in enumerate(rows):
+            run("y", [lambda e, n=n, m=m, j=j: e.dma_start(ap(R(n, 0, 128, 1, j, j + 1)), ap(P0(m)))],
+                [P0(m)], [R(n, 0, 128, 1, j, j + 1)], 2.0, dma=True)
+    ts(f("trc"), f("li"), f("b2"), O.add)
+    ms(R("kc", 0, 8), 4096.0)
+    ms(R("kc", 8, 16), 8192.0)
+    for t in range(2):
+        step[0] = t
+        ms(R("y", 0, 1), 0.0)
+        ms(R("x", 2048, 2320), 0.0)
+    for r in range(16):
+        keep(R("lr", 128 * r, 128 * r + 128), f("blk"), [[0, 8], [1, 16]], O.is_equal, 0.0, -r, 0)
+
+    def prep(t):
+        step[0] = t
+        tag[0] = "u%d" % (t > 0)
+        z, U = zb(t), R("pu", 0, 128)
+        mm([(U, f("whb"), z, True, False), (U, f("wlb"), z, False, True)])
+        tt(f("um"), U, R("m16", 0, 128), O.mult)
+        scan(f("us"), f("rs"), f("um"), O.mult, O.add)
+        cp(f("ui"), R("us", 15, 128, 16))
+        ts(f("ua"), f("ui"), 4095, O.bitwise_and)
+        ts(f("xq"), f("ua"), 592.0, O.add)
+        tt(f("sq"), f("xq"), f("xq"), O.mult)
+        ts(f("bs"), f("sq"), 5, O.arith_shift_right, 511, O.bitwise_and)
+        tag[0] = "zx%d" % (t > 0)
+        for k in range(16):
+            if t and k < GK:
+                keep(R("zx", k, 2048, 16), z, [[0, 128]], O.is_gt, 0.0, 1, 0)
+            elif t == 0 and k < VK:
+                cp(R("zx", k, 2048, 16), z)
+            else:
+                act(R("zx", k, 2048, 16), z)
+        tag[0] = "dup%d" % (t > 0)
+        if t < 3:
+            ts(f("u8"), f("ui"), 255, O.bitwise_and)
+            cp(f("ul"), f("u8"))
+            act(f("ub"), f("ubt", f("ul")))
+        cp(f("bl"), f("bs"))
+        act(f("fe"), f("ft", f("bl")), scale=f("b3"))
+        act(f("fo"), f("ft", f("bl")), scale=f("b7"))
+        for a in range(4):
+            ps, l = ("p1", "p2")[a & 1], []
+            for j, fx in enumerate(("fe", "fo")):
+                x = R(fx, 0, 128, 1, 32 * a, 32 * a + 32)
+                l.append((R(ps, 128 * j, 128 * j + 128), x, x, True, True))
+            mm(l)
+            act(R("e1", 256 * a, 256 * a + 256), R(ps, 0, 256), AF.Relu, bias=-15.0)
+        mm([(R("pu", 256 + 16 * j, 272 + 16 * j), R("e1", 128 * j, 128 * j + 128), f("wm"), True, True) for j in range(8)])
+        tt(f("dl"), R("pu", 256, 384), f("m16w"), O.mult)
+        mm([(R("pu", 384, 392), f("dl"), f("rb"), True, True)])
+        ts(f("du"), R("pu", 384, 392), 0.625, O.is_ge, 1024.0, O.mult)
+        tt(f("dtr"), f("du"), f("trc"), O.min)
+
+    KEY, BP = R("pk", 0, 128), R("p6", 0, 128)
+
+    def front(t):
+        step[0] = t
+        tag[0] = "host%d" % (t > 0)
+        if t == 0:
+            ts(f("vt"), f("bs"), 312.0, O.add)
+        else:
+            ts(f("vt"), f("bs"), R("p4", 128, 129), O.add, 312.0, O.add)
+        ts(f("vi"), f("vt"), 511, O.bitwise_and)
+        cp(f("vl"), f("vi"))
+        cp(f("bo"), R("btab", 0, 512, off=f("vl")))
+        act(f("bg"), R("btab", 0, 512, off=f("vl")))
+        one = R("onb", 0, 128, 1, 0, 1)
+        mm([(KEY, R("k3l", 0, 128, 1, 0, 3), R("k3r", 0, 128, 1, 0, 3), True, False)], grp="key%d" % t)
+        mm([(BP, R("onf", 0, 128, 1, 0, 1), R("newr", 128 * t, 128 * t + 128, 1, 0, 1), True, False)], grp="bp%d" % t)
+        tag[0] = "chunk%d" % (t > 0)
+        for c in range(4):
+            x = R("x", 512 * c, 512 * c + 512)
+            ab = [R("ab", 512 * c + k, 512 * c + 512, 16) for k in range(16)]
+            bo = R("bo", 32 * c, 32 * c + 32)
+            tt(x, R("gz", 0, 2048 + 128 * t, off=bo), R("zx", 512 * c, 512 * c + 512), O.subtract)
+            act(R("ab", 512 * c, 512 * c + 512), x, AF.Abs)
+            mm([(R("pk", k, 128, 16, 32 * c, 32 * c + 32), ab[k], f("bd"), False, False) for k in range(16)], grp="key%d" % t)
+        tag[0] = "st"
+        if t:
+            keep(R("gz", t, 2048, 16), zb(t), [[0, 128]], O.is_gt, 0.0, 1, 0)
+        else:
+            act(R("gz", t, 2048, 16), zb(t))
+        act(f("qg"), R("qtab", 0, 512, off=f("vl")))
+        act(f("pq"), f("qg"), AF.Relu, bias=float(t + 1), scale=-1.0)
+        W = R("p5", 0, 128)
+        mm([(W, one, R("crow", 0, 128, 1, 0, 1), True, False), (W, f("qg"), f("i16"), False, True)])
+        scan(f("sw"), f("rs"), W, O.mult, O.min)
+        tt(f("gL"), f("sw", R("bco", 0, 8)), R("m16", 0, 128), O.mult)
+        G0 = R("p5", 128, 136)
+        mm([(G0, f("gL"), f("rb"), True, False), (G0, R("rrow", 0, 128, 1, 0, 1), R("onb", 0, 8, 1, 0, 1), False, False),
+            (G0, one, R("qrow", 0, 8, 1, 0, 1), False, True)])
+        tag[0] = "sick"
+        act(f("ig"), R("itab", 0, 512, off=f("vl")))
+        mm([(R("p4", 384, 512), f("ident"), zb(t), True, False), (R("p4", 384, 512), f("nid"), f("ig"), False, True)])
+        act(f("gs"), R("p4", 384, 512), AF.Sign, bias=-0.5)
+        mm([(R("p4", 0, 128), f("blk"), f("gs"), True, True)])
+        act(f("pen"), R("p4", 0, 128), AF.Relu, bias=1.0, scale=-1.0)
+        mm([(KEY, f("pq"), f("bigi"), False, False), (KEY, f("pen"), f("bigi"), False, True)], grp="key%d" % t)
+        tag[0] = "top"
+        scan(R("ss", 0, 128), f("rs"), KEY, O.mult, O.min)
+        tt(R("y", 1, 128), R("ss", 0, 127), R("pk", 1, 128), O.max)
+        scan(R("ss", 128, 256), f("y"), f("rs"), O.min, O.mult)
+        tag[0] = "awake"
+        if t < 4:
+            act(f("sg"), R("ss", 15, 256, 16), AF.Sign, accum=f("ac"))
+            mm([(R("p4", 128, 129), f("onn"), f("ac"), True, True)])
+        tag[0] = "rows"
+        tt(f("L"), f("ss", f("bco")), f("m16"), O.mult)
+        mm([(R("p5", 136 + j, 144 + j), R("L", 16 * j, 16 * j + 128), f("rf"), True, True) for j in (0, 8)])
+        ts(f("mi"), R("p5", 136, 152), 2304.0, O.add)
+        ts(f("Z"), f("mi"), 4095, O.bitwise_and)
+        tt(f("Zm"), R("Z", 0, 8), R("Z", 8, 16), O.min)
+        tt(f("G"), f("Zm"), R("p5", 128, 136), O.min)
+        cp(f("gl"), f("G"))
+        act(f("oh"), f("oht", f("gl")))
+        mm([(BP, f("ident"), f("oh"), False, True)], grp="bp%d" % t)
+        tt(f("oi"), f("vi"), f("dtr"), O.max)
+        cp(f("ol"), f("oi"))
+        tt(f("bn"), f("bg"), BP, O.max)
+        cp(R("btab", 0, 640, off=f("ol")), f("bn"))
+
+    def back(t):
+        step[0] = t
+        tag[0] = "stw"
+        z, idn = zb(t), f("ident")
+        cp(f("xl"), f("Z"))
+        act(f("za"), f("zt", f("xl")))
+        act(f("oq"), f("oh"), AF.Relu, bias=8.0 + t, scale=(8 + t) / 8192.0)
+        QP = R("p2", 256, 384)
+        mm([(QP, idn, f("qg"), True, False), (QP, idn, R("za", 0, 128), False, False), (QP, idn, R("za", 128, 256), False, True)])
+        tt(f("qn"), QP, f("oq"), O.max)
+        cp(R("qtab", 0, 640, off=f("ol")), f("qn"))
+        tag[0] = "post"
+        act(R("X", 0, 256), f("x", f("xl")))
+        tt(R("X", 256, 384), R("X", 128, 256), R("X", 0, 128), O.subtract)
+        ts(R("cm", 0, 384), f("X"), 0.0, O.is_gt)
+        ts(R("cm", 384, 768), f("X"), 0.0, O.is_lt)
+        mm([(R("p3", 0, 48), R("lr", 128 * r, 128 * r + 128), R("cm", r, 768, 16), r == 0, r == 15) for r in range(16)])
+        ts(f("pz"), R("Z", 8, 16), 2304.0, O.is_ge, 65536.0, O.mult)
+        tt(f("oK"), f("Z"), f("kc"), O.add)
+        ts(f("bb"), R("p3", 0, 48), 9.0, O.is_ge, 16384.0, O.mult)
+        K = lambda j, l=1: R("K", 8 * j, 8 * j + 8 * l)
+        P = lambda j, l=1: R("p3", 48 + 8 * j, 48 + 8 * j + 8 * l)
+        B = lambda j, l=1: R("bb", 8 * j, 8 * j + 8 * l)
+        m = lambda j: R("mm", 8 * j, 8 * j + 8)
+        mm([(P(0), R("onb", 0, 128, 1, 0, 1), R("c23", 0, 8, 1, 0, 1), True, False), (P(0), idn, B(0), False, False), (P(0), idn, B(1), False, True)])
+        mm([(P(1, 2), f("idf"), f("oK"), True, False), (P(1, 2), idn, B(3, 2), False, False), (P(1), idn, B(2), False, False),
+            (P(2), idn, f("pz"), False, False), (P(2), idn, B(5), False, True)])
+        act(K(0, 3), P(0, 3))
+        tt(m(0), K(0), K(1), O.min)
+        tt(m(1), K(0), K(1), O.max)
+        tt(m(2), m(1), K(2), O.min)
+        tt(R("fm", 0, 8), m(0), K(2), O.min)
+        tt(R("fm", 8, 16), m(0), m(2), O.max)
+        ts(f("fa"), f("fm"), 4095, O.bitwise_and)
+        cp(f("fl"), f("fa"))
+        act(f("xf"), f("x", f("fl")))
+        tag[0] = "cross"
+        if t < 3:
+            d, c = R("p1", 256, 384), R("p1", 384, 512)
+            mm([(d, idn, R("xf", 0, 128), True, False), (d, f("nid"), R("xf", 128, 256), False, True)])
+            tt(f("db"), d, f("ub"), O.mult)
+            mm([(c, idn, z, True, False), (c, idn, R("xf", 128, 256), False, False), (c, idn, f("db"), False, True)])
+            act(f("cr%d" % t), c)
+            send(T.cores[(rank + 2) % N], t + 2, f("cr%d" % t))
+        tag[0] = "imm"
+        FP = R("p4", 256, 384)
+        act(f("im1"), f("ig"), AF.Identity, bias=-1.0)
+        mm([(FP, idn, z, True, False), (FP, idn, R("xf", 0, 128), False, True)])
+        tt(f("inn"), FP, f("im1"), O.max)
+        cp(R("itab", 0, 640, off=f("ol")), f("inn"))
+
+    prep(0)
+    for t in range(5):
+        front(t)
+        if t == 0:
+            prep(1)
+        elif t < 4:
+            prep(t + 1)
+        back(t)
+    tag[0] = "end"
+    store("y", T.ygeno[:], R("gz", 0, 2048))
+    for j in (0, 1):
+        a, b = 256 * j, 256 * j + 256
+        act(R("q2", a, b), R("qtab", a, b), AF.Copy, scale=2048.0)
+        ts(R("bki", a, b), R("btab", a, b), 4096.0, O.mult)
+        ts(R("bt0", a, b), R("bki", a, b), 4095, O.bitwise_and)
+        tt(R("yb", a, b), R("bt0", a, b), R("q2", a, b), O.add)
+        store("y", T.ybank[:, a:b], R("yb", a, b))
+    store("y", T.yimm[:], R("itab", 0, 512))
+
+    def clash(r, w, r2, w2):
+        if r[3] == r2[3] > 1 and (r[1] - r2[1]) % r[3]:
+            return False
+        return (w or w2) and r[1] < r2[2] and r2[1] < r[2] and r[4] < r2[5] and r2[4] < r[5]
+
+    pred, seen = [], {}
+    for k, o in enumerate(ops):
+        p = {o["after"]} if "after" in o else set()
+        for r, w in o["regs"]:
+            for k2, r2, w2 in seen.get(r[0], ()):
+                if k2 not in p and clash(r, w, r2, w2):
+                    p.add(k2)
+        for r, w in o["regs"]:
+            seen.setdefault(r[0], []).append((k, r, w))
+        pred.append(p)
+    succ = [[] for _ in ops]
+    for k, p in enumerate(pred):
+        for k2 in p:
+            succ[k2].append(k)
+    way = [0.0] * len(ops)
+    for k in range(len(ops) - 1, -1, -1):
+        way[k] = ops[k]["cost"] + max([WAKE + way[j] for j in succ[k]] + [0.0])
+    way = [w + BONUS.get(o["tag"], 0.0) for w, o in zip(way, ops)]
+    left = [len(p) for p in pred]
+    ready = [k for k in range(len(ops)) if not left[k]]
+    end, free, bank, order = [0.0] * len(ops), {}, {}, []
+    while ready:
+        best = {}
+        at = {}
+        for k in ready:
+            o = ops[k]
+            s = free.get(o["q"], 0.0)
+            for j in pred[k]:
+                s = max(s, end[j] + WAKE)
+            for r, w in o["regs"]:
+                if r[0] in PS:
+                    for q, e in bank.get(r[0], {}).items():
+                        if q != o["q"]:
+                            s = max(s, e + WAKE)
+            at[k] = s
+            hold = 0.1 if o.get("dma") else o["cost"]
+            q = o["q"]
+            best[q] = min(best.get(q, 1e9), s + hold)
+        q = min((at[k], ops[k]["q"]) for k in ready)[1]
+        k = max((way[k], -k) for k in ready if ops[k]["q"] == q and at[k] < best[q])
+        k = -k[1]
+        o = ops[k]
+        ready.remove(k)
+        order.append(k)
+        end[k] = at[k] + o["cost"]
+        if q != "net":
+            free[q] = at[k] + (0.1 if o.get("dma") else o["cost"])
+        for r, w in o["regs"]:
+            if r[0] in PS:
+                bank.setdefault(r[0], {})[q] = end[k]
+        for j in succ[k]:
+            left[j] -= 1
+            if not left[j]:
+                ready.append(j)
+
+    know = {q: 0 for q in eng}
+    know["net"] = 0
+    done, semof, acc, chains, used = {}, {}, {}, [], {"c": 0, "d": 0}
+    for n, k in enumerate(order):
+        o = ops[k]
+        q, grp = o["q"], o.get("grp")
+        if q == "net":
+            done[k], semof[k] = 1 << k, o["sem"]
+        else:
+            need = set()
+            for r, w in o["regs"]:
+                for k2, q2, r2, w2, g2 in acc.get(r[0], ()):
+                    if know[q] >> k2 & 1 or (grp is not None and g2 == grp):
+                        continue
+                    if (r[0] in PS and q2 != q) or clash(r, w, r2, w2):
+                        need.add((-order.index(k2), k2))
+            for _, k2 in sorted(need):
+                if not know[q] >> k2 & 1:
+                    eng[q].wait_ge(T.sem[semof[k2][0]], semof[k2][1])
+                    know[q] |= done[k2]
+            done[k] = know[q] | 1 << k
+            if o.get("dma"):
+                nm = "d%d" % used["d"]
+                used["d"] += 1
+                semof[k] = (nm, 16)
+                chains.append([nm, 16, k, False])
+                o["calls"][0](eng[q]).then_inc(T.sem[nm], 16)
+            elif "sem" in o:
+                semof[k] = o["sem"]
+                o["calls"][0](eng[q])
+            else:
+                ch = None
+                for c in chains:
+                    if c[3] and know[q] >> c[2] & 1:
+                        ch = c
+                        break
+                if ch is None:
+                    ch = ["c%d" % used["c"], 0, k, True]
+                    used["c"] += 1
+                    chains.append(ch)
+                ch[1] += len(o["calls"])
+                ch[2] = k
+                semof[k] = (ch[0], ch[1])
+                for c in o["calls"]:
+                    c(eng[q]).then_inc(T.sem[ch[0]], 1)
+        for r, w in o["regs"]:
+            acc.setdefault(r[0], []).append((k, q, r, w, grp))
+    for nm, val, _, _ in chains:
+        g.wait_ge(T.sem[nm], val)
+    for nm, val in lands:
+        g.wait_ge(T.sem[nm], val)
+    g.wait_ge(T.sem["snd"], sent[0])

@@ -2,40 +2,39 @@ from concourse.mybir import AluOpType as O, AxisListType, ActivationFunctionType
 
 BF, F4, I4, U2 = "bfloat16", "float32", "int32", "uint16"
 SIZE = {BF: 2, U2: 2, F4: 4, I4: 4}
+PAD = 2240
+XW = PAD + 256
 ONE = {
     "gz": (2688, BF), "zb1": (128, BF), "bki": (512, I4), "bt0": (512, I4), "btab": (640, F4), "qtab": (640, BF), "itab": (640, BF),
-    "wti": (1, I4), "wlo": (1, I4), "whi": (1, I4), "wlof": (1, F4), "whif": (1, F4),
-    "m16": (256, F4), "ident": (128, BF), "idf": (128, F4), "nid": (128, BF), "tri": (128, BF), "tz": (128, BF), "blk": (128, BF),
-    "blk0": (128, BF), "hot": (128, BF), "pi": (1, I4), "bd": (8, BF), "rf0": (8, F4), "rf": (8, F4), "rb": (8, BF), "r1k": (8, BF),
-    "lr": (2048, BF), "whb": (128, BF), "wlb": (128, BF), "rs": (128, F4), "bcf": (16, F4), "bco": (16, U2), "onb": (128, BF),
-    "onf": (128, F4), "onn": (128, F4), "c6k": (128, BF), "c23": (16, BF), "crow": (128, BF), "lrow": (128, BF), "rrow": (128, BF), "qrow": (8, BF),
-    "oht": (2304, BF), "zt": (2320, BF), "iv": (256, I4), "c2": (1, F4), "c8": (1, F4), "qr": (512, F4), "qm": (512, F4), "ft": (512, BF), "ubt": (256, BF), "uv2": (256, I4), "uv2b": (256, I4), "pw": (16, F4),
-    "half": (16, F4), "zero": (16, F4), "li": (8, I4), "trc": (8, I4), "kc": (16, F4),
-    "newr": (640, F4), "irow": (128, F4), "chalf": (128, BF), "ctwo": (128, BF), "wrow": (128, BF),
-    "vrow": (128, BF), "wm": (16, BF), "m16w": (128, F4), "k3l": (128, BF), "k3r": (128, BF), "bigi": (128, BF), "i16": (128, BF),
-    "cr0": (128, BF), "cr1": (128, BF), "cr2": (128, BF), "yb": (512, F4), "q2": (512, F4),
+    "wti": (1, I4), "wlo": (1, I4), "whi": (1, I4), "wlof": (1, F4), "whif": (1, F4), "whb": (128, BF), "wlb": (128, BF),
+    "onb": (160, BF), "idw": (160, BF), "ie": (160, BF), "io": (160, BF), "nid": (128, BF), "nid2": (128, BF), "i2k": (128, BF),
+    "blk": (128, BF), "blk0": (128, BF), "hot": (128, BF), "hotb": (128, BF), "iper": (128, BF), "nbp": (128, BF),
+    "ld": (144, BF), "lc": (144, BF), "rs": (128, BF), "r1": (128, BF), "kc": (128, BF), "onn": (128, F4),
+    "oht": (XW, BF), "onf": (256, BF), "iv": (256, F4), "qr": (512, F4), "qm": (512, F4), "ft": (512, BF), "ubt": (256, BF),
+    "uv2": (256, I4), "uv2b": (256, I4), "pw": (16, F4), "half": (16, F4), "zero": (16, F4), "m16": (16, F4),
+    "li": (8, I4), "trc": (8, I4), "four": (8, BF), "lt4": (8, BF), "wc0": (8, BF), "wc": (8, BF), "ordr": (24, BF), "sev": (48, BF),
+    "newr": (640, F4), "cr0": (128, BF), "cr1": (128, BF), "cr2": (128, BF), "yb": (512, F4),
 }
-for _i in range(8):
-    ONE["a%d" % _i] = (1, I4)
-    ONE["b%d" % _i] = (1, F4)
+for _k in ("even", "odd", "e16", "o16", "rr", "r16", "b6", "b5", "c2", "c8", "pr", "thr"):
+    ONE[_k] = (1, F4)
+for _i in range(4):
     ONE["h%d" % _i] = (16, F4)
 TWO = {
-    "um": (128, F4), "us": (128, F4), "ui": (8, I4), "ua": (8, I4), "u8": (8, I4), "xq": (8, F4), "sq": (8, I4), "bs": (8, I4),
-    "ul": (8, U2), "bl": (8, U2), "fe": (128, BF), "fo": (128, BF), "e1": (1024, BF), "dl": (128, BF), "du": (8, F4), "dtr": (8, I4),
-    "zx": (2048, BF), "x": (2320, BF), "ab": (2048, BF), "bo": (128, U2), "bg": (128, F4), "qg": (128, BF),
-    "ig": (128, BF), "ub": (128, BF), "vt": (8, I4), "vi": (8, I4), "vl": (8, U2), "oi": (8, I4), "ol": (8, U2),
-    "ss": (256, F4), "y": (128, F4), "sg": (16, F4), "ac": (1, F4), "L": (256, F4), "sw": (128, F4), "gL": (128, BF), "mi": (16, I4),
-    "Z": (16, I4), "Zm": (8, I4), "G": (8, I4), "gl": (8, U2), "oh": (128, BF), "za": (256, BF), "oq": (128, BF),
-    "bn": (128, F4), "qn": (128, BF), "inn": (128, BF), "im1": (128, BF), "xl": (16, U2),
-    "pz": (8, BF), "oK": (16, F4), "gs": (128, BF), "pen": (128, BF), "pq": (128, BF), "X": (384, BF), "cm": (768, BF),
-    "bb": (48, BF), "K": (24, F4), "mm": (24, F4), "fm": (16, I4), "fa": (16, I4), "fl": (16, U2), "xf": (256, BF),
-    "db": (128, BF),
+    "us": (128, F4), "ui": (8, I4), "ua": (8, I4), "xq": (8, F4), "sq": (8, I4), "bu": (16, I4), "bl": (16, U2),
+    "fe": (128, BF), "fo": (128, BF), "du": (8, F4), "dtr": (8, I4), "x": (XW, BF), "bo": (128, U2), "bg": (128, F4),
+    "qg": (128, BF), "qp": (128, BF), "tq": (128, BF), "pq": (128, BF), "pen": (128, BF), "tp": (128, BF),
+    "ig": (128, BF), "gs": (128, BF), "im1": (128, BF), "ub": (256, BF), "vt": (8, I4), "vi": (8, I4), "vl": (8, U2),
+    "ss": (256, F4), "y": (128, F4), "sg": (16, F4), "ac": (1, F4), "sw": (128, F4), "G0": (8, F4), "mi": (16, I4),
+    "Z": (40, I4), "Zm": (8, I4), "xl": (32, U2), "nv": (128, F4), "za": (384, BF), "qn": (128, BF), "inn": (128, BF),
+    "X": (384, BF), "cm": (768, BF), "bb": (48, BF), "K": (24, F4), "mm": (24, F4), "fm": (16, I4), "fa": (16, I4),
+    "fl": (16, U2), "xf": (256, BF), "db": (256, BF), "zx": (2048, BF),
 }
-_OWN = ("gz", "zb1", "bki", "btab", "qtab", "itab", "wti", "yb", "cr0", "cr1", "cr2", "x", "zx", "ab", "oht", "zt", "k3l", "k3r")
-SCRATCH, PLACE, STRIDE, _fill = {}, {}, {}, {BF: 0, F4: 0, I4: 0, U2: 0}
+CUBE = {"ab": (8, 256, BF), "e1": (8, 128, BF)}
+_OWN = ("gz", "zb1", "bki", "btab", "qtab", "itab", "wti", "yb", "cr0", "cr1", "cr2", "x", "oht")
+SCRATCH, PLACE, STRIDE, DTYPE, _fill = {}, {}, {}, {}, {BF: 0, F4: 0, I4: 0, U2: 0}
 for _t, _m in ((ONE, 1), (TWO, 2)):
     for _k, (_n, _d) in _t.items():
-        STRIDE[_k] = -(-_n // 16) * 16
+        STRIDE[_k], DTYPE[_k] = -(-_n // 16) * 16, _d
         if _k in _OWN:
             SCRATCH[_k] = ("sbuf", [128, STRIDE[_k] * _m if _m == 2 else _n], _d)
             PLACE[_k] = (_k, 0)
@@ -44,15 +43,18 @@ for _t, _m in ((ONE, 1), (TWO, 2)):
             _fill[_d] += STRIDE[_k] * _m
 for _d, _n in _fill.items():
     SCRATCH["all_" + _d] = ("sbuf", [128, _n], _d)
-PS = ("pk", "pu", "p1", "p2", "p3", "p4", "p5", "p6")
+for _k, (_a, _n, _d) in CUBE.items():
+    SCRATCH[_k] = ("sbuf", [128, 2 * _a, _n], _d)
+    DTYPE[_k] = _d
+PS = ("k0", "k1", "d0", "d1", "pu", "pi", "pc", "px")
 for _k in PS:
-    SCRATCH[_k] = ("psum", [128, 512], F4)
-    PLACE[_k] = (_k, 0)
-SEMAPHORES = ["c%d" % _i for _i in range(100)] + ["d%d" % _i for _i in range(40)] + ["rz1", "rz2", "rz3", "rz4", "snd"]
-NET = [5.0, 3.0]
-GK, VK = 8, 8
-BONUS = {"cross": 2.0, "imm": 8.0, "sick": 2.0, "host0": 2.0, "dup1": -4.0, "top": -4.0, "u1": -2.0}
-WAKE = 0.09
+    SCRATCH[_k] = ("psum", [128, 16, 32] if _k[0] == "d" else [128, 512], F4)
+    PLACE[_k], DTYPE[_k] = (_k, 0), F4
+SEMAPHORES = ["c%d" % _i for _i in range(118)] + ["d%d" % _i for _i in range(26)] + ["rz1", "rz2", "rz3", "rz4", "snd"]
+CYC, GATH, SCAT, WAKE, DMA, NET, FIRST = 0.001, 1.5, 3.5, 0.08, 2.2, 3.0, 3.5
+CHUNKS = ((0, 2), (2, 4), (4, 6), (6, 7), (7, 8))
+OPT = dict(z0=(16, 0), z1=(10, 0), x3s=0, immv=1, crv=0, sick=1, qs=1)
+BONUS = {}
 
 
 def rank_program(g, core, T, topo):
@@ -65,404 +67,432 @@ def rank_program(g, core, T, topo):
     step = [0]
     tag = ["set"]
 
+    def comb(a, b, st):
+        return sum(1 << j for j in range(a, b, st)) if st > 1 else (1 << b) - (1 << a)
+
     def R(n, a, b, st=1, p0=0, p1=128, off=None):
         if n in TWO:
             a, b = a + (step[0] & 1) * STRIDE[n], b + (step[0] & 1) * STRIDE[n]
-        return (n, a, b, st, p0, p1, off)
+        m, c = PLACE[n]
+        x = T[m][p0:p1, c + a:c + b] if st == 1 else T[m][p0:p1, c + a:c + b:st]
+        if off:
+            return (n, comb(a, b, st), p0, p1, x.indirect(off[4]), 16 * off[5], off)
+        return (n, comb(a, b, st), p0, p1, x, len(range(a, b, st)), None)
+
+    def C(n, i, j, a, b):
+        w = SCRATCH[n][1][2]
+        s = (step[0] & 1) * CUBE[n][0] if n in CUBE else 0
+        rows = range(s + i, s + (i + 1 if j is None else j))
+        x = T[n][:, s + i, a:b] if j is None else T[n][:, s + i:s + j, a:b]
+        return (n, sum(comb(w * r + a, w * r + b, 1) for r in rows), 0, 128, x, len(rows) * (b - a), None)
 
     def f(n, off=None):
         return R(n, 0, (TWO[n] if n in TWO else ONE[n])[0], off=off)
 
-    def ap(r):
-        n, a, b, st, p0, p1, off = r
-        n, c = PLACE[n]
-        x = T[n][p0:p1, c + a:c + b] if st == 1 else T[n][p0:p1, c + a:c + b:st]
-        return x.indirect(ap(off)) if off else x
-
-    def wide(r):
-        return 16 * (r[6][2] - r[6][1]) if r[6] else -(-(r[2] - r[1]) // r[3])
-
     def small(*rs):
-        return all(r[0] not in PS and (TWO[r[0]] if r[0] in TWO else ONE[r[0]])[1] in (BF, U2) for r in rs)
+        return all(SIZE[DTYPE[r[0]]] == 2 for r in rs)
 
     def run(q, calls, reads, writes, cost, **kw):
         regs = [(r, 0) for r in reads] + [(r, 1) for r in writes] + [(r[6], 0) for r in list(reads) + list(writes) if r[6]]
-        ops.append(dict(q=q, calls=calls, regs=regs, cost=cost, tag=tag[0], **kw))
+        ops.append(dict(q=q, calls=calls, regs=regs, cost=cost, tag=tag[0], step=step[0], **kw))
         return len(ops) - 1
 
-    def vcost(n, o, ins):
-        if o[6]:
-            return 0.05 + 3.5 * wide(o) * 0.00083
-        if any(isinstance(a, tuple) and a[6] for a in ins):
-            return 0.05 + 1.5 * wide(o) * 0.00083
-        return 0.02 + max(64, n) * 0.001
+    def vcost(n, o, a):
+        if o[6] or (a and a[6]):
+            return 0.07 + (SCAT if o[6] else GATH) * o[5] * CYC
+        return max(64, n) * CYC
+
+    def val(s):
+        return s[4] if isinstance(s, tuple) else s
 
     def tt(o, a, b, op):
-        n = wide(o) * (1 if a[0] in PS or b[0] in PS else 2)
-        run("v", [lambda e: e.tensor_tensor(ap(o), ap(a), ap(b), op)], [a, b], [o], vcost(n, o, [a]))
+        n = o[5] * (1 if a[0] in PS or b[0] in PS else 2)
+        run("v", [lambda e: e.tensor_tensor(o[4], a[4], b[4], op)], [a, b], [o], vcost(n, o, a))
 
     def ts(o, a, s1, op0, s2=None, op1=None):
         rd = [a] + [s for s in (s1, s2) if isinstance(s, tuple)]
-        val = lambda s: ap(s) if isinstance(s, tuple) else s
-        c = vcost(wide(o) * (0.5 if small(o, a) else 1), o, [a])
+        c = vcost(o[5] * (0.5 if small(o, a) else 1), o, a)
         if op1 is None:
-            run("v", [lambda e: e.tensor_scalar(ap(o), ap(a), val(s1), None, op0)], rd, [o], c)
+            run("v", [lambda e: e.tensor_scalar(o[4], a[4], val(s1), None, op0)], rd, [o], c)
         else:
-            run("v", [lambda e: e.tensor_scalar(ap(o), ap(a), val(s1), val(s2), op0, op1)], rd, [o], c)
+            run("v", [lambda e: e.tensor_scalar(o[4], a[4], val(s1), val(s2), op0, op1)], rd, [o], c)
 
     def cp(o, a):
-        run("v", [lambda e: e.tensor_copy(ap(o), ap(a))], [a], [o], vcost(wide(o) * (0.5 if small(o, a) else 1), o, [a]))
+        run("v", [lambda e: e.tensor_copy(o[4], a[4])], [a], [o], vcost(o[5] * (0.5 if small(o, a) else 1), o, a))
+
+    def turn(o, a):
+        run("v", [lambda e: e.transpose(o[4], a[4])], [a], [o], vcost(o[5] * 0.5, o, a))
 
     def scan(o, a, b, op0, op1, init=0.0):
-        run("v", [lambda e: e.tensor_tensor_scan(ap(o), ap(a), ap(b), init, op0, op1)], [a, b], [o], vcost(wide(o), o, []))
+        run("v", [lambda e: e.tensor_tensor_scan(o[4], a[4], b[4], init, op0, op1)], [a, b], [o], vcost(o[5], o, None))
 
     def red(o, a):
-        run("v", [lambda e: e.tensor_reduce(ap(o), ap(a), AxisListType.X, O.add)], [a], [o], vcost(wide(a), o, []))
+        run("v", [lambda e: e.tensor_reduce(o[4], a[4], AxisListType.X, O.add)], [a], [o], vcost(a[5], o, None))
 
     def ms(o, c):
-        run("v", [lambda e: e.memset(ap(o), c)], [], [o], vcost(wide(o) * (0.5 if small(o) else 1), o, []))
+        run("v", [lambda e: e.memset(o[4], c)], [], [o], vcost(o[5] * (0.5 if small(o) else 1), o, None))
 
-    def act(o, a, fn=AF.Copy, bias=None, scale=None, accum=None):
-        kw = {}
-        for nm, val in (("bias", bias), ("scale", scale), ("accum_out", accum)):
-            if val is not None:
-                kw[nm] = val
-
-        def call(e):
-            return e.activation(ap(o), ap(a), fn, **{m: ap(v) if isinstance(v, tuple) else v for m, v in kw.items()})
-        run("s", [call], [a] + [v for v in (bias, scale) if isinstance(v, tuple)], [o] + ([accum] if accum else []), vcost(wide(o), o, [a]) + 0.01)
+    def act(o, a, fn=AF.Copy, **kw):
+        rd = [a] + [kw[m] for m in ("bias", "scale") if isinstance(kw.get(m), tuple)]
+        run("s", [lambda e: e.activation(o[4], a[4], fn, **{m: val(v) for m, v in kw.items()})], rd,
+            [o] + ([kw["accum_out"]] if "accum_out" in kw else []), vcost(o[5], o, a))
 
     def mm(lst, grp=None):
-        c = 0.02
-        for z in lst:
-            m = wide(z[1])
-            c += max(min(64, m), wide(z[2])) * 0.001 * (1 if small(z[1]) else 4)
-        run("t", [lambda e, z=z: e.matmul(ap(z[0]), ap(z[1]), ap(z[2]), z[3], z[4]) for z in lst],
+        c = sum(max(min(64, z[1][5]), z[2][5]) * CYC * (1 if small(z[1]) else 4) for z in lst)
+        run("t", [lambda e, z=z: e.matmul(z[0][4], z[1][4], z[2][4], z[3], z[4]) for z in lst],
             [z[1] for z in lst] + [z[2] for z in lst], [z[0] for z in lst], c, grp=grp)
+
+    def sums(o, terms, grp=None):
+        return [(o, a, b, j == 0, j == len(terms) - 1) for j, (a, b) in enumerate(terms)]
 
     def iota(o, pat, base, cm, whole=True):
         kw = {} if whole else {"allow_small_or_imprecise_dtypes": True}
-        run("g", [lambda e: e.iota(ap(o), pat, base, cm, **kw)], [], [o], 0.13 + 0.002 * wide(o))
+        run("g", [lambda e: e.iota(o[4], pat, base, cm, **kw)], [], [o], 0.16 + 2 * CYC * o[5])
 
     def keep(o, a, pat, cmp, fill, base, cm):
-        run("g", [lambda e: e.affine_select(ap(o), ap(a), pat, cmp, fill, base, cm)], [a], [o], 0.17 + 0.002 * wide(o))
+        run("g", [lambda e: e.affine_select(o[4], a[4], pat, cmp, fill, base, cm)], [a], [o], 0.2 + 2 * CYC * o[5])
 
-    def load(q, o, src):
-        run(q, [lambda e: e.dma_start(ap(o), src)], [], [o], 2.0 + (wide(o) * SIZE[ONE[o[0]][1]] * 128) / 200e3, dma=True)
+    def gcopy(o, a):
+        keep(o, a, [[0, o[5]]], O.is_gt, 0.0, 1, 0)
 
-    def store(q, dst, a):
-        run(q, [lambda e: e.dma_start(dst, ap(a))], [a], [], 2.0, dma=True)
+    def dma(q, o, a):
+        r = o if isinstance(o, tuple) else a
+        run(q, [lambda e: e.dma_start(val(o), val(a))], [a] if isinstance(a, tuple) else [], [o] if isinstance(o, tuple) else [],
+            DMA + r[5] * SIZE[DTYPE[r[0]]] * 128 / 220e3, hold=0.06, dma=True)
 
     sent, lands = [0], []
 
+    def zb(t):
+        return R("gz", 2048 + 128 * t, 2176 + 128 * t)
+
     def send(dst, t, a):
-        o, rsem = R("gz", 2048 + 128 * t, 2176 + 128 * t), "rz%d" % t
+        o, rsem = zb(t), "rz%d" % t
         rid, pid = topo.addr(dst, core)
         m, ne = 0, 0
         for e in topo.engines(core, dst)[:8]:
             m, ne = m | 1 << e, ne + 1
         sent[0] += ne
-        k = run("g", [lambda e: e.remote_dma(ap(o), ap(a), T.sem[rsem], T.sem["snd"], pid, rid, m)], [a], [], 0.5, sem=("snd", sent[0]))
+        k = run("g", [lambda e: e.remote_dma(o[4], a[4], T.sem[rsem], T.sem["snd"], pid, rid, m)], [a], [],
+                0.3 if lands else 0.3 + FIRST, sem=("snd", sent[0]))
         src = T.cores[(2 * rank - T.rank_of(dst)) % N]
         n = len(topo.engines(src, core)[:8])
-        run("net", [], [], [o], NET[0] if lands else NET[0] + NET[1], sem=(rsem, n), after=k)
+        run("net", [], [], [o], NET, sem=(rsem, n), after=k)
         lands.append((rsem, n))
 
-    def zb(t):
-        return R("gz", 2048 + 128 * t, 2176 + 128 * t)
-
-    load("y", f("wti"), T.wt[:])
-    load("s", zb(0), T.bites[:, 0:128])
-    load("s", f("zb1"), T.bites[:, 128:256])
-    load("y", f("bki"), T.bank[:])
-    load("y", R("gz", 0, 1024), T.geno[:, 0:1024])
-    load("s", R("gz", 1024, 2048), T.geno[:, 1024:2048])
-    load("y", R("itab", 0, 512), T.immun[:])
+    dma("y", f("wti"), T.wt[:])
+    dma("s", zb(0), T.bites[:, 0:128])
+    dma("y", f("bki"), T.bank[:])
+    dma("s", f("zb1"), T.bites[:, 128:256])
+    dma("y", R("gz", 0, 1024), T.geno[:, 0:1024])
+    dma("s", R("gz", 1024, 2048), T.geno[:, 1024:2048])
+    dma("y", R("itab", 0, 512), T.immun[:])
+    tag[0] = "send1"
     send(T.cores[(rank + 1) % N], 1, f("zb1"))
+    tag[0] = "set"
 
-    iota(f("pi"), [[0, 1]], 0, 1)
+    one, idn, rb = R("onb", 0, 128), R("idw", 16, 144), R("blk", 0, 128, 16)
+    row = lambda n, a, b, p=0: R(n, a, b, 1, p, p + 1)
     ms(f("onb"), 1.0)
-    ms(f("onf"), 1.0)
-    ms(f("tz"), 0.0)
-    keep(f("hot"), f("onb"), [[0, 8], [-1, 16]], O.is_equal, 0.0, 0, 1)
-    keep(f("blk0"), f("onb"), [[-16, 8], [0, 16]], O.is_ge, 0.0, 0, 1)
+    keep(f("blk0"), one, [[-16, 8], [0, 16]], O.is_ge, 0.0, 0, 1)
     keep(f("blk"), f("blk0"), [[16, 8], [0, 16]], O.is_ge, 0.0, 15, -1)
-    keep(f("rs"), f("onf"), [[0, 8], [1, 16]], O.is_gt, 0.0, 0, 0)
-    keep(f("rf0"), R("onf", 0, 8), [[-16, 8]], O.is_ge, 0.0, 0, 1)
-    keep(f("rf"), f("rf0"), [[16, 8]], O.is_ge, 0.0, 15, -1)
-    keep(f("ident"), f("onb"), [[-1, 128]], O.is_equal, 0.0, 0, 1)
-    keep(f("idf"), f("onf"), [[-1, 128]], O.is_equal, 0.0, 0, 1)
-    iota(f("bcf"), [[16, 16]], 15, 0, False)
-    iota(f("iv"), [[1, 256]], 0, 0)
-    iota(f("irow"), [[1, 128]], 0, 0, False)
-    iota(f("crow"), [[0, 8], [1, 16]], -256, 0, False)
-    iota(f("lrow"), [[16, 128]], 0, 0, False)
-    iota(f("rrow"), [[0, 8], [16, 16]], 0, 0, False)
-    iota(f("qrow"), [[256, 8]], 256, 0, False)
+    keep(f("hot"), one, [[0, 8], [-1, 16]], O.is_equal, 0.0, 0, 1)
+    keep(f("idw"), f("onb"), [[-1, 160]], O.is_equal, 0.0, 16, 1)
+    keep(f("iper"), one, [[-32, 4], [-1, 16], [-16, 2]], O.is_equal, 0.0, 0, 1)
+    iota(R("kc", 0, 128, 1, 0, 2), [[256, 8], [0, 16]], -PAD - 4096, 0, False)
+    iota(row("kc", 0, 128), [[0, 8], [1, 16]], 0, 0, False)
     iota(f("li"), [[16, 8]], 512, 0)
-
-    def part(j, op, val):
-        ts(f("a%d" % j), f("pi"), val, op)
-        cp(f("b%d" % j), f("a%d" % j))
-
-    part(2, O.bitwise_and, 15)
-    part(4, O.bitwise_and, 16)
+    ms(f("four"), 4.0)
+    keep(f("lt4"), f("four"), [[16, 8]], O.is_gt, 0.0, 0, -1)
     ts(f("wlo"), f("wti"), 63, O.bitwise_and)
     ts(f("whi"), f("wti"), 4032, O.bitwise_and)
     cp(f("wlof"), f("wlo"))
     cp(f("whif"), f("whi"))
     act(f("wlb"), f("blk"), scale=f("wlof"))
-    act(f("whb"), f("blk"), scale=f("whif"))
-    mm([(R("p1", 0, 128), f("hot"), f("hot"), True, True)])
+    ts(f("whb"), f("blk"), f("whif"), O.mult)
+    act(f("hotb"), f("hot"), scale=-4194304.0)
+    for n, a, b in (("rs", 1.0, 0.0), ("r1", -1e9, 1.0)):
+        ms(f(n), a)
+        ms(R(n, 0, 128, 16), b)
+    for n, c in (("ld", -4096.0), ("lc", 1.0)):
+        ms(f(n), 0.0)
+        ts(R(n, 15, 143, 16), rb, c, O.mult)
+    mm([(R("px", 0, 128), f("hot"), f("hot"), True, True)])
+    act(f("m16"), R("px", 0, 16))
     for j in (0, 128):
-        act(R("m16", j, j + 128), R("p1", 0, 128))
-        act(R("zt", j, j + 128), R("p1", 0, 128), scale=-16.0)
-        act(R("oht", j, j + 128), R("p1", 0, 128), scale=8192.0, bias=-8192.0)
-    for n, a, w in (("oht", 256, 256), ("zt", 256, 256), ("oht", 512, 256), ("zt", 512, 256), ("oht", 768, 256), ("zt", 768, 256),
-                    ("oht", 2048, 256), ("oht", 1024, 1024), ("zt", 1024, 1024)):
-        run("y", [lambda e, n=n, a=a, w=w: e.dma_start(ap(R(n, a, a + w)), ap(R(n, 0, w)))],
-            [R(n, 0, w)], [R(n, a, a + w)], 2.3, dma=True)
-    ms(R("zt", 2048, 2320), 0.0)
-    act(f("rb"), f("rf"))
-    act(f("bd"), f("rf"), scale=-4096.0)
+        act(R("oht", j, j + 128), R("px", 0, 128))
+    for a, w in ((256, 256), (512, 256), (768, 256), (2048, PAD - 2048), (1024, 1024)):
+        dma("y", R("oht", a, a + w), R("oht", 0, w))
+    ms(R("oht", PAD, XW), 0.0)
     ts(f("bt0"), f("bki"), 2047, O.bitwise_and)
     ts(R("btab", 0, 512), f("bt0"), 4097.0 / 4096.0, O.mult)
     ts(f("qr"), f("bki"), -1023.5, O.add, 1.0 / 2048, O.mult)
     act(f("qm"), f("qr"), AF.Identity, bias=12582912.0)
     act(R("qtab", 0, 512), f("qm"), AF.Identity, bias=-12582912.0)
-    ms(f("onn"), -1.0)
-    ms(f("c6k"), -6144.0)
-    ms(f("c23"), 2304.0)
-    act(f("bigi"), f("ident"), scale=8388608.0)
-    act(f("i16"), f("ident"), scale=16.0)
-    act(f("nid"), f("ident"), scale=-1.0)
-    cp(f("bco"), f("bcf"))
+    ms(f("onn"), -0.5)
+    act(f("nid"), idn, scale=-1.0)
+    act(f("nid2"), idn, scale=-2.0)
+    act(f("i2k"), idn, scale=2048.0)
+    mm([(R("px", 128, 256), f("blk"), f("iper"), True, True)])
+    act(f("nbp"), R("px", 128, 256), scale=-1.0)
+    red(f("even"), R("blk", 0, 128, 32))
+    red(f("odd"), R("blk", 16, 128, 32))
+    ts(f("e16"), f("even"), 16.0, O.mult)
+    ts(f("o16"), f("odd"), 16.0, O.mult)
+    act(f("ie"), f("idw"), scale=f("e16"))
+    act(f("io"), f("idw"), scale=f("o16"))
+    turnto = ((R("ie", 16, 144), R("ie", 0, 128)), (R("io", 32, 160), R("io", 16, 144)))
+    ms(f("onf"), 1.0)
+    scan(f("iv"), f("onf"), f("onf"), O.mult, O.add, -1.0)
     for t in range(5):
-        act(R("newr", 128 * t, 128 * t + 128, 1, 0, 1), R("irow", 0, 128, 1, 0, 1), AF.Copy, scale=1.0 + 16 / 4096.0,
-            bias=2048.0 + 128 * t + t / 4096.0)
+        act(R("newr", 128 * t, 128 * t + 128), R("iv", 0, 128), AF.Copy, scale=1.0 + 16 / 4096.0, bias=2048.0 + 128 * t + t / 4096.0)
+
+    def column(n, j, a):
+        tt(f("h%d" % j), f("m16"), a, O.mult)
+        red(f(n), f("h%d" % j))
+
+    column("rr", 1, R("iv", 0, 16))
+    ts(f("r16"), f("rr"), 16.0, O.mult, float(PAD), O.add)
+    ts(f("trc"), f("li"), f("rr"), O.add)
     ms(f("half"), 0.5)
     ms(f("zero"), 0.0)
     scan(f("pw"), f("half"), f("zero"), O.mult, O.add, 1024.0)
     for j in (0, 8):
         cp(R("h0", j, j + 8), R("pw", 0, 8))
-    tt(f("h1"), R("m16", 0, 16), f("h0"), O.mult)
-    red(f("b6"), f("h1"))
+    column("b6", 2, f("h0"))
     ts(f("uv2"), f("iv"), f("b6"), O.mult)
     ts(f("uv2b"), f("uv2"), 512, O.bitwise_and)
     ts(f("ubt"), f("uv2b"), 1.0 / 512, O.mult)
-    ts(f("b3"), f("b4"), -1.0 / 16, O.mult, 1.0, O.add)
-    ts(f("b7"), f("b4"), 1.0 / 16, O.mult)
     red(f("b5"), R("m16", 0, 8))
     act(f("c2"), f("b5"), scale=2.0)
     act(f("c8"), R("m16", 8, 9), scale=2.0, bias=-1.0)
     act(R("ft", 0, 256), f("ubt"), AF.Identity, scale=f("c2"), bias=-1.0)
     act(R("ft", 256, 512), f("ubt"), AF.Identity, scale=f("c2"), bias=f("c8"))
-    ms(f("chalf"), 0.5)
-    ms(f("ctwo"), 2.0)
-    P0 = lambda n: R(n, 0, 128, 1, 0, 1)
-    scan(P0("wrow"), P0("chalf"), P0("tz"), O.mult, O.add, 2.0 ** 64)
-    scan(P0("vrow"), P0("ctwo"), P0("tz"), O.mult, O.add, 2.0 ** -66)
-    mm([(R("p2", 0, 16), P0("wrow"), R("onb", 0, 16, 1, 0, 1), True, True), (R("p2", 16, 17), P0("vrow"), R("onb", 0, 1, 1, 0, 1), True, True)])
-    act(f("wm"), R("p2", 0, 16))
-    act(f("b1"), R("p2", 16, 17))
-    act(f("m16w"), R("m16", 0, 128), scale=f("b1"))
-    for n, rows in (("k3l", ("onb", "lrow", "onb")), ("k3r", ("crow", "onb", "c6k"))):
-        for j, m in enumerate(rows):
-            run("y", [lambda e, n=n, m=m, j=j: e.dma_start(ap(R(n, 0, 128, 1, j, j + 1)), ap(P0(m)))],
-                [P0(m)], [R(n, 0, 128, 1, j, j + 1)], 2.0, dma=True)
-    ts(f("trc"), f("li"), f("b2"), O.add)
-    ms(R("kc", 0, 8), 4096.0)
-    ms(R("kc", 8, 16), 8192.0)
+    column("pr", 3, f("pw"))
+    ts(f("thr"), f("pr"), 2.5, O.mult)
+    ts(f("wc0"), rb, f("pr"), O.mult)
+    ts(f("lt4"), f("lt4"), 512.0, O.mult)
+    tt(f("wc"), f("wc0"), f("lt4"), O.add)
+    for j in range(3):
+        ms(row("ordr", 8 * j, 8 * j + 8), 4096.0 * j)
+    if OPT["x3s"]:
+        ms(row("sev", 0, 32), 0.0)
+        ms(row("sev", 32, 48), 7.0)
     for t in range(2):
         step[0] = t
-        ms(R("y", 0, 1), 0.0)
-        ms(R("x", 2048, 2320), 0.0)
-    for r in range(16):
-        keep(R("lr", 128 * r, 128 * r + 128), f("blk"), [[0, 8], [1, 16]], O.is_equal, 0.0, -r, 0)
+        ms(R("y", 0, 128, 64), 0.0)
+        ms(R("x", 2048, XW), 0.0)
+        ms(R("x", PAD, XW, 16), -128.0)
+        ms(R("Z", 0, 8), PAD + 1)
 
     def prep(t):
         step[0] = t
-        tag[0] = "u%d" % (t > 0)
+        tag[0] = "u"
         z, U = zb(t), R("pu", 0, 128)
-        mm([(U, f("whb"), z, True, False), (U, f("wlb"), z, False, True)])
-        tt(f("um"), U, R("m16", 0, 128), O.mult)
-        scan(f("us"), f("rs"), f("um"), O.mult, O.add)
+        top16 = lambda n: R(n, 0, 128, 1, 0, 16)
+        mm(sums(U, [(top16("hot"), top16("hotb")), (f("whb"), z), (f("wlb"), z)]))
+        scan(f("us"), f("rs"), U, O.mult, O.min)
         cp(f("ui"), R("us", 15, 128, 16))
         ts(f("ua"), f("ui"), 4095, O.bitwise_and)
         ts(f("xq"), f("ua"), 592.0, O.add)
         tt(f("sq"), f("xq"), f("xq"), O.mult)
-        ts(f("bs"), f("sq"), 5, O.arith_shift_right, 511, O.bitwise_and)
-        tag[0] = "zx%d" % (t > 0)
+        ts(R("bu", 0, 8), f("sq"), 5, O.arith_shift_right, 511, O.bitwise_and)
+        tag[0] = "zx"
+        zs, zv = OPT["z0"] if t == 0 else OPT["z1"]
         for k in range(16):
-            if t and k < GK:
-                keep(R("zx", k, 2048, 16), z, [[0, 128]], O.is_gt, 0.0, 1, 0)
-            elif t == 0 and k < VK:
-                cp(R("zx", k, 2048, 16), z)
-            else:
-                act(R("zx", k, 2048, 16), z)
-        tag[0] = "dup%d" % (t > 0)
+            (act if k < zs else cp if k < zs + zv else gcopy)(R("zx", k, 2048, 16), z)
+        tag[0] = "dup"
         if t < 3:
-            ts(f("u8"), f("ui"), 255, O.bitwise_and)
-            cp(f("ul"), f("u8"))
-            act(f("ub"), f("ubt", f("ul")))
-        cp(f("bl"), f("bs"))
-        act(f("fe"), f("ft", f("bl")), scale=f("b3"))
-        act(f("fo"), f("ft", f("bl")), scale=f("b7"))
+            ts(R("bu", 8, 16), f("ui"), 255, O.bitwise_and)
+            cp(f("bl"), f("bu"))
+            act(R("ub", 0, 128), f("ubt", R("bl", 8, 16)))
+            if OPT["crv"]:
+                act(R("ub", 128, 256), R("ub", 0, 128), scale=-1.0, bias=1.0)
+        else:
+            cp(R("bl", 0, 8), R("bu", 0, 8))
+        act(f("fe"), f("ft", R("bl", 0, 8)), scale=f("even"))
+        act(f("fo"), f("ft", R("bl", 0, 8)), scale=f("odd"))
         for a in range(4):
-            ps, l = ("p1", "p2")[a & 1], []
+            ps, l = ("d0", "d1")[a & 1], []
             for j, fx in enumerate(("fe", "fo")):
                 x = R(fx, 0, 128, 1, 32 * a, 32 * a + 32)
-                l.append((R(ps, 128 * j, 128 * j + 128), x, x, True, True))
+                l.append((C(ps, 0, 8, 16 * j, 16 * j + 16), x, x, True, True))
             mm(l)
-            act(R("e1", 256 * a, 256 * a + 256), R(ps, 0, 256), AF.Relu, bias=-15.0)
-        mm([(R("pu", 256 + 16 * j, 272 + 16 * j), R("e1", 128 * j, 128 * j + 128), f("wm"), True, True) for j in range(8)])
-        tt(f("dl"), R("pu", 256, 384), f("m16w"), O.mult)
-        mm([(R("pu", 384, 392), f("dl"), f("rb"), True, True)])
-        ts(f("du"), R("pu", 384, 392), 0.625, O.is_ge, 1024.0, O.mult)
+            act(C("e1", 0, 8, 32 * a, 32 * a + 32), C(ps, 0, 8, 0, 32), AF.Relu, bias=-15.0)
+        mm([(R("pu", 128 + c, 129 + c), C("e1", c, None, 0, 128), R("wc", c, c + 1), True, True) for c in range(8)])
+        ts(f("du"), R("pu", 128, 136), f("thr"), O.is_ge, 1024.0, O.mult)
         tt(f("dtr"), f("du"), f("trc"), O.min)
 
-    KEY, BP = R("pk", 0, 128), R("p6", 0, 128)
+    KEY = [R("k0", 0, 64), R("k1", 0, 64)]
+    half = lambda n, h: R(n, 64 * h, 64 * h + 64)
+    A = R("pu", 384, 385)
 
     def front(t):
         step[0] = t
-        tag[0] = "host%d" % (t > 0)
+        tag[0] = "host"
+        z = zb(t)
         if t == 0:
-            ts(f("vt"), f("bs"), 312.0, O.add)
+            ts(f("vt"), R("bu", 0, 8), 312.0, O.add)
         else:
-            ts(f("vt"), f("bs"), R("p4", 128, 129), O.add, 312.0, O.add)
+            ts(f("vt"), R("bu", 0, 8), A, O.add, 1336.0, O.add)
         ts(f("vi"), f("vt"), 511, O.bitwise_and)
         cp(f("vl"), f("vi"))
+        tag[0] = "bo"
         cp(f("bo"), R("btab", 0, 512, off=f("vl")))
         act(f("bg"), R("btab", 0, 512, off=f("vl")))
-        one = R("onb", 0, 128, 1, 0, 1)
-        mm([(KEY, R("k3l", 0, 128, 1, 0, 3), R("k3r", 0, 128, 1, 0, 3), True, False)], grp="key%d" % t)
-        mm([(BP, R("onf", 0, 128, 1, 0, 1), R("newr", 128 * t, 128 * t + 128, 1, 0, 1), True, False)], grp="bp%d" % t)
-        tag[0] = "chunk%d" % (t > 0)
-        for c in range(4):
-            x = R("x", 512 * c, 512 * c + 512)
-            ab = [R("ab", 512 * c + k, 512 * c + 512, 16) for k in range(16)]
-            bo = R("bo", 32 * c, 32 * c + 32)
-            tt(x, R("gz", 0, 2048 + 128 * t, off=bo), R("zx", 512 * c, 512 * c + 512), O.subtract)
-            act(R("ab", 512 * c, 512 * c + 512), x, AF.Abs)
-            mm([(R("pk", k, 128, 16, 32 * c, 32 * c + 32), ab[k], f("bd"), False, False) for k in range(16)], grp="key%d" % t)
+        const = lambda h: (R("onb", 0, 128, 1, 0, 2), R("kc", 64 * h, 64 * h + 64, 1, 0, 2))
+        for h in (0, 1):
+            mm([(KEY[h],) + const(h) + (True, False)], grp="key%d%d" % (t, h))
+        tag[0] = "chunk"
+        for a, b in CHUNKS:
+            x = R("x", 256 * a, 256 * b)
+            tt(x, R("gz", 0, 2048 + 128 * t, off=R("bo", 16 * a, 16 * b)), R("zx", 256 * a, 256 * b), O.subtract)
+            act(C("ab", a, b, 0, 256), x, AF.Abs)
+            if b in (4, 8):
+                h = b // 4 - 1
+                mm([(KEY[h], R("ld", 15 - r, 143 - r), C("ab", 4 * h, 4 * h + 4, 16 * r, 16 * r + 16), False, False) for r in range(16)],
+                   grp="key%d%d" % (t, h))
         tag[0] = "st"
-        if t:
-            keep(R("gz", t, 2048, 16), zb(t), [[0, 128]], O.is_gt, 0.0, 1, 0)
-        else:
-            act(R("gz", t, 2048, 16), zb(t))
+        gcopy(R("gz", t, 2048, 16), z)
         act(f("qg"), R("qtab", 0, 512, off=f("vl")))
-        act(f("pq"), f("qg"), AF.Relu, bias=float(t + 1), scale=-1.0)
-        W = R("p5", 0, 128)
-        mm([(W, one, R("crow", 0, 128, 1, 0, 1), True, False), (W, f("qg"), f("i16"), False, True)])
-        scan(f("sw"), f("rs"), W, O.mult, O.min)
-        tt(f("gL"), f("sw", R("bco", 0, 8)), R("m16", 0, 128), O.mult)
-        G0 = R("p5", 128, 136)
-        mm([(G0, f("gL"), f("rb"), True, False), (G0, R("rrow", 0, 128, 1, 0, 1), R("onb", 0, 8, 1, 0, 1), False, False),
-            (G0, one, R("qrow", 0, 8, 1, 0, 1), False, True)])
+        act(f("pq"), f("qg"), AF.Relu, bias=32.0 * (t + 1), scale=-32.0)
+        mm([(C("d0", 8, 12, 16 * h, 16 * h + 16), f("iper"), half("qg", h), True, True) for h in (0, 1)])
+        act(f("qp"), C("d0", 8, 12, 0, 32))
+        turn(f("tq"), f("qp"))
+        W = lambda h: R("pu", 256 + 64 * h, 320 + 64 * h)
+        mm([m for h in (0, 1) for m in sums(W(h), [const(h)] + [(turnto[h][j], R("tq", j, 128, 2)) for j in (0, 1)])])
+        scan(f("sw"), f("rs"), R("pu", 256, 384), O.mult, O.min)
+        ts(f("G0"), R("sw", 15, 128, 16), f("r16"), O.add, 4096.0, O.add)
         tag[0] = "sick"
-        act(f("ig"), R("itab", 0, 512, off=f("vl")))
-        mm([(R("p4", 384, 512), f("ident"), zb(t), True, False), (R("p4", 384, 512), f("nid"), f("ig"), False, True)])
-        act(f("gs"), R("p4", 384, 512), AF.Sign, bias=-0.5)
-        mm([(R("p4", 0, 128), f("blk"), f("gs"), True, True)])
-        act(f("pen"), R("p4", 0, 128), AF.Relu, bias=1.0, scale=-1.0)
-        mm([(KEY, f("pq"), f("bigi"), False, False), (KEY, f("pen"), f("bigi"), False, True)], grp="key%d" % t)
-        tag[0] = "top"
-        scan(R("ss", 0, 128), f("rs"), KEY, O.mult, O.min)
-        tt(R("y", 1, 128), R("ss", 0, 127), R("pk", 1, 128), O.max)
-        scan(R("ss", 128, 256), f("y"), f("rs"), O.min, O.mult)
+        if OPT["sick"] == 0:
+            act(f("ig"), R("itab", 0, 512, off=f("vl")))
+            mm(sums(R("pi", 0, 128), [(idn, z), (f("nid"), f("ig"))]))
+            act(f("gs"), R("pi", 0, 128), AF.Sign, bias=-0.5)
+            if OPT["immv"]:
+                act(f("im1"), R("pi", 0, 128), scale=-1.0, bias=-1.0)
+            else:
+                act(f("im1"), f("ig"), bias=-1.0)
+        else:
+            tt(f("ig"), R("itab", 0, 512, off=f("vl")), z, O.subtract)
+            act(f("gs"), f("ig"), AF.Sign, bias=-0.5, scale=-1.0)
+            act(f("im1"), f("ig"), bias=-1.0)
+        mm([m for h in (0, 1) for m in sums(C("d1", 8, 12, 16 * h, 16 * h + 16), [(f("iper"), half("pq", h)), (f("nbp"), half("gs", h))])])
+        act(f("pen"), C("d1", 8, 12, 0, 32), AF.Relu, bias=524288.0, scale=524288.0)
+        turn(f("tp"), f("pen"))
+        for h in (0, 1):
+            tag[0] = "sick"
+            mm([(KEY[h], turnto[h][j], R("tp", j, 128, 2), False, j == 1) for j in (0, 1)], grp="key%d%d" % (t, h))
+            tag[0] = "top"
+            a = 64 * h
+            scan(R("ss", a, a + 64), R("r1", 0, 64), KEY[h], O.max, O.min)
+            tt(R("y", a + 1, a + 64), R("ss", a, a + 63), R("k%d" % h, 1, 64), O.max)
+            scan(R("ss", 128 + a, 192 + a), R("y", a, a + 64), R("rs", 0, 64), O.min, O.mult)
         tag[0] = "awake"
         if t < 4:
-            act(f("sg"), R("ss", 15, 256, 16), AF.Sign, accum=f("ac"))
-            mm([(R("p4", 128, 129), f("onn"), f("ac"), True, True)])
+            act(f("sg"), R("ss", 15, 256, 16), AF.Sign, bias=0.5, accum_out=f("ac"))
+            mm([(A, f("onn"), f("ac"), True, True)])
         tag[0] = "rows"
-        tt(f("L"), f("ss", f("bco")), f("m16"), O.mult)
-        mm([(R("p5", 136 + j, 144 + j), R("L", 16 * j, 16 * j + 128), f("rf"), True, True) for j in (0, 8)])
-        ts(f("mi"), R("p5", 136, 152), 2304.0, O.add)
-        ts(f("Z"), f("mi"), 4095, O.bitwise_and)
-        tt(f("Zm"), R("Z", 0, 8), R("Z", 8, 16), O.min)
-        tt(f("G"), f("Zm"), R("p5", 128, 136), O.min)
-        cp(f("gl"), f("G"))
-        act(f("oh"), f("oht", f("gl")))
-        mm([(BP, f("ident"), f("oh"), False, True)], grp="bp%d" % t)
-        tt(f("oi"), f("vi"), f("dtr"), O.max)
-        cp(f("ol"), f("oi"))
-        tt(f("bn"), f("bg"), BP, O.max)
-        cp(R("btab", 0, 640, off=f("ol")), f("bn"))
+        ts(f("mi"), R("ss", 15, 256, 16), f("r16"), O.add)
+        ts(R("Z", 8, 24), f("mi"), 4095, O.bitwise_and)
+        cp(R("xl", 0, 16), R("Z", 8, 24))
+        tt(f("Zm"), R("Z", 8, 16), R("Z", 16, 24), O.min)
+        tt(R("Z", 24, 32), f("Zm"), f("G0"), O.min)
+        tt(R("Z", 32, 40), f("vi"), f("dtr"), O.max)
+        cp(R("xl", 16, 32), R("Z", 24, 40))
+        tt(f("nv"), f("oht", R("xl", 16, 24)), R("newr", 128 * t, 128 * t + 128), O.mult)
+        tt(R("btab", 0, 640, off=R("xl", 24, 32)), f("bg"), f("nv"), O.max)
 
     def back(t):
         step[0] = t
         tag[0] = "stw"
-        z, idn = zb(t), f("ident")
-        cp(f("xl"), f("Z"))
-        act(f("za"), f("zt", f("xl")))
-        act(f("oq"), f("oh"), AF.Relu, bias=8.0 + t, scale=(8 + t) / 8192.0)
-        QP = R("p2", 256, 384)
-        mm([(QP, idn, f("qg"), True, False), (QP, idn, R("za", 0, 128), False, False), (QP, idn, R("za", 128, 256), False, True)])
-        tt(f("qn"), QP, f("oq"), O.max)
-        cp(R("qtab", 0, 640, off=f("ol")), f("qn"))
+        z, ol = zb(t), R("xl", 24, 32)
+        blk3 = lambda n, j, l=1: R(n, 128 * j, 128 * (j + l))
+        act(f("za"), f("oht", R("xl", 0, 24)), scale=8.0 + t)
+        QP = R("pi", 128, 256)
+        if OPT["qs"]:
+            mm(sums(QP, [(idn, f("qg"))] + [(f("nid2"), blk3("za", j)) for j in range(3)]))
+            act(f("qn"), QP, AF.Relu)
+            tt(R("qtab", 0, 640, off=ol), f("qn"), blk3("za", 2), O.add)
+        else:
+            mm(sums(QP, [(idn, f("qg"))] + [(f("nid2"), blk3("za", j)) for j in range(2)]))
+            tt(f("qn"), QP, blk3("za", 2), O.max)
+            cp(R("qtab", 0, 640, off=ol), f("qn"))
         tag[0] = "post"
-        act(R("X", 0, 256), f("x", f("xl")))
-        tt(R("X", 256, 384), R("X", 128, 256), R("X", 0, 128), O.subtract)
-        ts(R("cm", 0, 384), f("X"), 0.0, O.is_gt)
-        ts(R("cm", 384, 768), f("X"), 0.0, O.is_lt)
-        mm([(R("p3", 0, 48), R("lr", 128 * r, 128 * r + 128), R("cm", r, 768, 16), r == 0, r == 15) for r in range(16)])
-        ts(f("pz"), R("Z", 8, 16), 2304.0, O.is_ge, 65536.0, O.mult)
-        tt(f("oK"), f("Z"), f("kc"), O.add)
-        ts(f("bb"), R("p3", 0, 48), 9.0, O.is_ge, 16384.0, O.mult)
-        K = lambda j, l=1: R("K", 8 * j, 8 * j + 8 * l)
-        P = lambda j, l=1: R("p3", 48 + 8 * j, 48 + 8 * j + 8 * l)
-        B = lambda j, l=1: R("bb", 8 * j, 8 * j + 8 * l)
+        act(blk3("X", 0, 2), f("x", R("xl", 0, 16)))
+        ts(blk3("cm", 0), blk3("X", 0), 0.0, O.is_gt)
+        ts(blk3("cm", 1, 2), blk3("X", 0, 2), 0.0, O.is_lt)
+        CN = R("pc", 128, 176)
+        cnt = [(R("lc", 15 - r, 143 - r), R("cm", r, 768, 16)) for r in range(16)]
+        if OPT["x3s"]:
+            ts(blk3("cm", 3), blk3("X", 1), 0.0, O.is_gt)
+            mm(sums(R("pc", 0, 128), [(idn, blk3("X", 1)), (f("nid"), blk3("X", 0))]))
+            act(blk3("cm", 4), R("pc", 0, 128), AF.Sign, bias=-0.5)
+            act(blk3("cm", 5), R("pc", 0, 128), AF.Sign, bias=-0.5, scale=-1.0)
+            cnt = [(row("onb", 0, 128), row("sev", 0, 48))] + cnt
+        else:
+            tt(blk3("X", 2), blk3("X", 1), blk3("X", 0), O.subtract)
+            ts(blk3("cm", 3, 2), blk3("X", 1, 2), 0.0, O.is_gt)
+            ts(blk3("cm", 5), blk3("X", 2), 0.0, O.is_lt)
+        mm(sums(CN, cnt))
+        ts(f("bb"), CN, 9.0, O.is_ge, 16384.0, O.mult)
+        P = R("pc", 192, 216)
+        mm(sums(P, [(row("onb", 0, 128), row("ordr", 0, 24)), (idn, R("bb", 0, 24)), (idn, R("bb", 24, 48))]))
+        tt(f("K"), P, R("Z", 0, 24), O.add)
+        K = lambda j: R("K", 8 * j, 8 * j + 8)
         m = lambda j: R("mm", 8 * j, 8 * j + 8)
-        mm([(P(0), R("onb", 0, 128, 1, 0, 1), R("c23", 0, 8, 1, 0, 1), True, False), (P(0), idn, B(0), False, False), (P(0), idn, B(1), False, True)])
-        mm([(P(1, 2), f("idf"), f("oK"), True, False), (P(1, 2), idn, B(3, 2), False, False), (P(1), idn, B(2), False, False),
-            (P(2), idn, f("pz"), False, False), (P(2), idn, B(5), False, True)])
-        act(K(0, 3), P(0, 3))
         tt(m(0), K(0), K(1), O.min)
         tt(m(1), K(0), K(1), O.max)
         tt(m(2), m(1), K(2), O.min)
         tt(R("fm", 0, 8), m(0), K(2), O.min)
-        tt(R("fm", 8, 16), m(0), m(2), O.max)
-        ts(f("fa"), f("fm"), 4095, O.bitwise_and)
-        cp(f("fl"), f("fa"))
-        act(f("xf"), f("x", f("fl")))
+        w = 16 if t < 3 else 8
+        if t < 3:
+            tt(R("fm", 8, 16), m(0), m(2), O.max)
+        else:
+            ops.pop(-2), ops.pop(-2)
+        ts(R("fa", 0, w), R("fm", 0, w), 4095, O.bitwise_and)
+        cp(R("fl", 0, w), R("fa", 0, w))
+        if not (OPT["immv"] and (t > 2 or OPT["crv"])):
+            act(R("xf", 0, 16 * w), f("x", R("fl", 0, w)))
         tag[0] = "cross"
         if t < 3:
-            d, c = R("p1", 256, 384), R("p1", 384, 512)
-            mm([(d, idn, R("xf", 0, 128), True, False), (d, f("nid"), R("xf", 128, 256), False, True)])
-            tt(f("db"), d, f("ub"), O.mult)
-            mm([(c, idn, z, True, False), (c, idn, R("xf", 128, 256), False, False), (c, idn, f("db"), False, True)])
+            d, c = R("px", 0, 128), R("px", 128, 256)
+            if OPT["crv"]:
+                tt(f("db"), f("x", f("fl")), f("ub"), O.mult)
+                mm(sums(c, [(idn, z), (idn, blk3("db", 0)), (idn, blk3("db", 1))]))
+            else:
+                mm(sums(d, [(idn, blk3("xf", 0)), (f("nid"), blk3("xf", 1))]))
+                tt(blk3("db", 0), d, blk3("ub", 0), O.mult)
+                mm(sums(c, [(idn, z), (idn, blk3("xf", 1)), (idn, blk3("db", 0))]))
             act(f("cr%d" % t), c)
             send(T.cores[(rank + 2) % N], t + 2, f("cr%d" % t))
         tag[0] = "imm"
-        FP = R("p4", 256, 384)
-        act(f("im1"), f("ig"), AF.Identity, bias=-1.0)
-        mm([(FP, idn, z, True, False), (FP, idn, R("xf", 0, 128), False, True)])
-        tt(f("inn"), FP, f("im1"), O.max)
-        cp(R("itab", 0, 640, off=f("ol")), f("inn"))
+        if OPT["immv"]:
+            tt(f("inn"), f("x", R("fl", 0, 8)), f("im1"), O.max)
+            tt(R("itab", 0, 640, off=ol), f("inn"), z, O.add)
+        else:
+            FP = R("pi", 256, 384)
+            mm(sums(FP, [(idn, z), (idn, blk3("xf", 0))]))
+            tt(f("inn"), FP, f("im1"), O.max)
+            cp(R("itab", 0, 640, off=ol), f("inn"))
 
     prep(0)
     for t in range(5):
         front(t)
-        if t == 0:
-            prep(1)
-        elif t < 4:
+        if t < 4:
             prep(t + 1)
         back(t)
     tag[0] = "end"
-    store("y", T.ygeno[:], R("gz", 0, 2048))
+    dma("y", T.ygeno[:], R("gz", 0, 2048))
     for j in (0, 1):
         a, b = 256 * j, 256 * j + 256
-        act(R("q2", a, b), R("qtab", a, b), AF.Copy, scale=2048.0)
         ts(R("bki", a, b), R("btab", a, b), 4096.0, O.mult)
         ts(R("bt0", a, b), R("bki", a, b), 4095, O.bitwise_and)
-        tt(R("yb", a, b), R("bt0", a, b), R("q2", a, b), O.add)
-        store("y", T.ybank[:, a:b], R("yb", a, b))
-    store("y", T.yimm[:], R("itab", 0, 512))
+        mm([(R("k%d" % j, 0, 256), f("i2k"), R("qtab", a, b), True, True)])
+        tt(R("yb", a, b), R("k%d" % j, 0, 256), R("bt0", a, b), O.add)
+        dma("y", T.ybank[:, a:b], R("yb", a, b))
+    dma("s", T.yimm[:], R("itab", 0, 512))
 
     def clash(r, w, r2, w2):
-        if r[3] == r2[3] > 1 and (r[1] - r2[1]) % r[3]:
-            return False
-        return (w or w2) and r[1] < r2[2] and r2[1] < r[2] and r[4] < r2[5] and r2[4] < r[5]
+        return (w or w2) and r[1] & r2[1] and r[2] < r2[3] and r2[2] < r[3]
 
     pred, seen = [], {}
     for k, o in enumerate(ops):
@@ -486,31 +516,27 @@ def rank_program(g, core, T, topo):
     ready = [k for k in range(len(ops)) if not left[k]]
     end, free, bank, order = [0.0] * len(ops), {}, {}, []
     while ready:
-        best = {}
-        at = {}
+        best, at = {}, {}
         for k in ready:
             o = ops[k]
-            s = free.get(o["q"], 0.0)
+            q = o["q"]
+            s = free.get(q, 0.0)
             for j in pred[k]:
                 s = max(s, end[j] + WAKE)
             for r, w in o["regs"]:
-                if r[0] in PS:
-                    for q, e in bank.get(r[0], {}).items():
-                        if q != o["q"]:
-                            s = max(s, e + WAKE)
+                for q2, e in bank.get(r[0], {}).items():
+                    if q2 != q:
+                        s = max(s, e + WAKE)
             at[k] = s
-            hold = 0.1 if o.get("dma") else o["cost"]
-            q = o["q"]
-            best[q] = min(best.get(q, 1e9), s + hold)
+            best[q] = min(best.get(q, 1e9), s + o.get("hold", o["cost"]))
         q = min((at[k], ops[k]["q"]) for k in ready)[1]
-        k = max((way[k], -k) for k in ready if ops[k]["q"] == q and at[k] < best[q])
-        k = -k[1]
+        k = -max((way[k], -k) for k in ready if ops[k]["q"] == q and at[k] < best[q])[1]
         o = ops[k]
         ready.remove(k)
         order.append(k)
         end[k] = at[k] + o["cost"]
         if q != "net":
-            free[q] = at[k] + (0.1 if o.get("dma") else o["cost"])
+            free[q] = at[k] + o.get("hold", o["cost"])
         for r, w in o["regs"]:
             if r[0] in PS:
                 bank.setdefault(r[0], {})[q] = end[k]
@@ -520,9 +546,9 @@ def rank_program(g, core, T, topo):
                 ready.append(j)
 
     know = {q: 0 for q in eng}
-    know["net"] = 0
+    place = {k: n for n, k in enumerate(order)}
     done, semof, acc, chains, used = {}, {}, {}, [], {"c": 0, "d": 0}
-    for n, k in enumerate(order):
+    for k in order:
         o = ops[k]
         q, grp = o["q"], o.get("grp")
         if q == "net":
@@ -534,7 +560,7 @@ def rank_program(g, core, T, topo):
                     if know[q] >> k2 & 1 or (grp is not None and g2 == grp):
                         continue
                     if (r[0] in PS and q2 != q) or clash(r, w, r2, w2):
-                        need.add((-order.index(k2), k2))
+                        need.add((-place[k2], k2))
             for _, k2 in sorted(need):
                 if not know[q] >> k2 & 1:
                     eng[q].wait_ge(T.sem[semof[k2][0]], semof[k2][1])
@@ -566,8 +592,8 @@ def rank_program(g, core, T, topo):
                     c(eng[q]).then_inc(T.sem[ch[0]], 1)
         for r, w in o["regs"]:
             acc.setdefault(r[0], []).append((k, q, r, w, grp))
-    for nm, val, _, _ in chains:
-        g.wait_ge(T.sem[nm], val)
-    for nm, val in lands:
-        g.wait_ge(T.sem[nm], val)
+    for nm, n, _, _ in chains:
+        g.wait_ge(T.sem[nm], n)
+    for nm, n in lands:
+        g.wait_ge(T.sem[nm], n)
     g.wait_ge(T.sem["snd"], sent[0])

from concourse.mybir import AluOpType as O, AxisListType, ActivationFunctionType as AF

BF, F4, I4, U2 = "bfloat16", "float32", "int32", "uint16"
SIZE = {BF: 2, U2: 2, F4: 4, I4: 4}
PAD = 2240
XW = PAD + 256
ONE = {
    "gz": (2688, BF), "zb1": (128, BF), "bki": (512, I4), "bt0": (512, I4), "btab": (640, F4), "qtab": (640, BF), "itab": (640, BF),
    "wti": (1, I4), "wlo": (1, I4), "whi": (1, I4), "wlof": (1, F4), "whif": (1, F4), "whb": (128, BF), "wlb": (128, BF),
    "onb": (160, BF), "idw": (160, BF), "ie": (160, BF), "io": (160, BF), "nid": (128, BF), "nid2": (128, BF), "i2k": (128, BF),
    "blk": (128, BF), "blk0": (128, BF), "hot": (128, BF), "hotb": (128, BF), "iper": (128, BF), "nbp": (128, BF),
    "ld": (144, BF), "lc": (144, BF), "rs": (128, BF), "r1": (128, BF), "kc": (128, BF), "onn": (128, F4),
    "oht": (XW, BF), "onf": (256, BF), "iv": (256, F4), "qr": (512, F4), "qm": (512, F4), "ft": (512, BF), "ubt": (256, BF),
    "uv2": (256, I4), "uv2b": (256, I4), "pw": (16, F4), "half": (16, F4), "zero": (16, F4), "m16": (16, F4),
    "li": (8, I4), "trc": (8, I4), "four": (8, BF), "lt4": (8, BF), "wc0": (8, BF), "wc": (8, BF), "ordr": (24, BF), "sev": (48, BF),
    "newr": (640, F4), "cr0": (128, BF), "cr1": (128, BF), "cr2": (128, BF), "yb": (512, F4),
}
for _k in ("even", "odd", "e16", "o16", "rr", "r16", "b6", "b5", "c2", "c8", "pr", "thr"):
    ONE[_k] = (1, F4)
for _i in range(4):
    ONE["h%d" % _i] = (16, F4)
TWO = {
    "us": (128, F4), "ui": (8, I4), "ua": (8, I4), "xq": (8, F4), "sq": (8, I4), "bu": (16, I4), "bl": (16, U2),
    "fe": (128, BF), "fo": (128, BF), "du": (8, F4), "dtr": (8, I4), "x": (XW, BF), "bo": (128, U2), "bg": (128, F4),
    "qg": (128, BF), "qp": (128, BF), "tq": (128, BF), "pq": (128, BF), "pen": (128, BF), "tp": (128, BF),
    "ig": (128, BF), "gs": (128, BF), "im1": (128, BF), "ub": (256, BF), "vt": (8, I4), "vi": (8, I4), "vl": (8, U2),
    "ss": (256, F4), "y": (128, F4), "sg": (16, F4), "ac": (1, F4), "sw": (128, F4), "G0": (8, F4), "mi": (16, I4),
    "Z": (40, I4), "Zm": (8, I4), "xl": (32, U2), "nv": (128, F4), "za": (384, BF), "qn": (128, BF), "inn": (128, BF),
    "X": (384, BF), "cm": (768, BF), "bb": (48, BF), "K": (24, F4), "mm": (24, F4), "fm": (16, I4), "fa": (16, I4),
    "fl": (16, U2), "xf": (256, BF), "db": (256, BF), "zx": (2048, BF),
}
CUBE = {"ab": (8, 256, BF), "e1": (8, 128, BF)}
_OWN = ("gz", "zb1", "bki", "btab", "qtab", "itab", "wti", "yb", "cr0", "cr1", "cr2", "x", "oht")
SCRATCH, PLACE, STRIDE, DTYPE, _fill = {}, {}, {}, {}, {BF: 0, F4: 0, I4: 0, U2: 0}
for _t, _m in ((ONE, 1), (TWO, 2)):
    for _k, (_n, _d) in _t.items():
        STRIDE[_k], DTYPE[_k] = -(-_n // 16) * 16, _d
        if _k in _OWN:
            SCRATCH[_k] = ("sbuf", [128, STRIDE[_k] * _m if _m == 2 else _n], _d)
            PLACE[_k] = (_k, 0)
        else:
            PLACE[_k] = ("all_" + _d, _fill[_d])
            _fill[_d] += STRIDE[_k] * _m
for _d, _n in _fill.items():
    SCRATCH["all_" + _d] = ("sbuf", [128, _n], _d)
for _k, (_a, _n, _d) in CUBE.items():
    SCRATCH[_k] = ("sbuf", [128, 2 * _a, _n], _d)
    DTYPE[_k] = _d
PS = ("k0", "k1", "d0", "d1", "pu", "pi", "pc", "px")
for _k in PS:
    SCRATCH[_k] = ("psum", [128, 16, 32] if _k[0] == "d" else [128, 512], F4)
    PLACE[_k], DTYPE[_k] = (_k, 0), F4
SEMAPHORES = ["c%d" % _i for _i in range(118)] + ["d%d" % _i for _i in range(26)] + ["rz1", "rz2", "rz3", "rz4", "snd"]
CYC, GATH, SCAT, WAKE, DMA, NET, FIRST = 0.001, 1.5, 3.5, 0.08, 2.2, 3.0, 3.5
CHUNKS = ((0, 2), (2, 4), (4, 6), (6, 7), (7, 8))
OPT = dict(z0=(16, 0), z1=(10, 0), x3s=0, immv=1, crv=0, sick=1, qs=1)
BONUS = {}


def rank_program(g, core, T, topo):
    rank = T.rank_of(core)
    if rank is None:
        return
    N = len(T.cores)
    eng = {"v": g.vector, "s": g.scalar, "t": g.tensor, "g": g, "y": g.sync}
    ops = []
    step = [0]
    tag = ["set"]

    def comb(a, b, st):
        return sum(1 << j for j in range(a, b, st)) if st > 1 else (1 << b) - (1 << a)

    def R(n, a, b, st=1, p0=0, p1=128, off=None):
        if n in TWO:
            a, b = a + (step[0] & 1) * STRIDE[n], b + (step[0] & 1) * STRIDE[n]
        m, c = PLACE[n]
        x = T[m][p0:p1, c + a:c + b] if st == 1 else T[m][p0:p1, c + a:c + b:st]
        if off:
            return (n, comb(a, b, st), p0, p1, x.indirect(off[4]), 16 * off[5], off)
        return (n, comb(a, b, st), p0, p1, x, len(range(a, b, st)), None)

    def C(n, i, j, a, b):
        w = SCRATCH[n][1][2]
        s = (step[0] & 1) * CUBE[n][0] if n in CUBE else 0
        rows = range(s + i, s + (i + 1 if j is None else j))
        x = T[n][:, s + i, a:b] if j is None else T[n][:, s + i:s + j, a:b]
        return (n, sum(comb(w * r + a, w * r + b, 1) for r in rows), 0, 128, x, len(rows) * (b - a), None)

    def f(n, off=None):
        return R(n, 0, (TWO[n] if n in TWO else ONE[n])[0], off=off)

    def small(*rs):
        return all(SIZE[DTYPE[r[0]]] == 2 for r in rs)

    def run(q, calls, reads, writes, cost, **kw):
        regs = [(r, 0) for r in reads] + [(r, 1) for r in writes] + [(r[6], 0) for r in list(reads) + list(writes) if r[6]]
        ops.append(dict(q=q, calls=calls, regs=regs, cost=cost, tag=tag[0], step=step[0], **kw))
        return len(ops) - 1

    def vcost(n, o, a):
        if o[6] or (a and a[6]):
            return 0.07 + (SCAT if o[6] else GATH) * o[5] * CYC
        return max(64, n) * CYC

    def val(s):
        return s[4] if isinstance(s, tuple) else s

    def tt(o, a, b, op):
        n = o[5] * (1 if a[0] in PS or b[0] in PS else 2)
        run("v", [lambda e: e.tensor_tensor(o[4], a[4], b[4], op)], [a, b], [o], vcost(n, o, a))

    def ts(o, a, s1, op0, s2=None, op1=None):
        rd = [a] + [s for s in (s1, s2) if isinstance(s, tuple)]
        c = vcost(o[5] * (0.5 if small(o, a) else 1), o, a)
        if op1 is None:
            run("v", [lambda e: e.tensor_scalar(o[4], a[4], val(s1), None, op0)], rd, [o], c)
        else:
            run("v", [lambda e: e.tensor_scalar(o[4], a[4], val(s1), val(s2), op0, op1)], rd, [o], c)

    def cp(o, a):
        run("v", [lambda e: e.tensor_copy(o[4], a[4])], [a], [o], vcost(o[5] * (0.5 if small(o, a) else 1), o, a))

    def turn(o, a):
        run("v", [lambda e: e.transpose(o[4], a[4])], [a], [o], vcost(o[5] * 0.5, o, a))

    def scan(o, a, b, op0, op1, init=0.0):
        run("v", [lambda e: e.tensor_tensor_scan(o[4], a[4], b[4], init, op0, op1)], [a, b], [o], vcost(o[5], o, None))

    def red(o, a):
        run("v", [lambda e: e.tensor_reduce(o[4], a[4], AxisListType.X, O.add)], [a], [o], vcost(a[5], o, None))

    def ms(o, c):
        run("v", [lambda e: e.memset(o[4], c)], [], [o], vcost(o[5] * (0.5 if small(o) else 1), o, None))

    def act(o, a, fn=AF.Copy, **kw):
        rd = [a] + [kw[m] for m in ("bias", "scale") if isinstance(kw.get(m), tuple)]
        run("s", [lambda e: e.activation(o[4], a[4], fn, **{m: val(v) for m, v in kw.items()})], rd,
            [o] + ([kw["accum_out"]] if "accum_out" in kw else []), vcost(o[5], o, a))

    def mm(lst, grp=None):
        c = sum(max(min(64, z[1][5]), z[2][5]) * CYC * (1 if small(z[1]) else 4) for z in lst)
        run("t", [lambda e, z=z: e.matmul(z[0][4], z[1][4], z[2][4], z[3], z[4]) for z in lst],
            [z[1] for z in lst] + [z[2] for z in lst], [z[0] for z in lst], c, grp=grp)

    def sums(o, terms, grp=None):
        return [(o, a, b, j == 0, j == len(terms) - 1) for j, (a, b) in enumerate(terms)]

    def iota(o, pat, base, cm, whole=True):
        kw = {} if whole else {"allow_small_or_imprecise_dtypes": True}
        run("g", [lambda e: e.iota(o[4], pat, base, cm, **kw)], [], [o], 0.16 + 2 * CYC * o[5])

    def keep(o, a, pat, cmp, fill, base, cm):
        run("g", [lambda e: e.affine_select(o[4], a[4], pat, cmp, fill, base, cm)], [a], [o], 0.2 + 2 * CYC * o[5])

    def gcopy(o, a):
        keep(o, a, [[0, o[5]]], O.is_gt, 0.0, 1, 0)

    def dma(q, o, a):
        r = o if isinstance(o, tuple) else a
        run(q, [lambda e: e.dma_start(val(o), val(a))], [a] if isinstance(a, tuple) else [], [o] if isinstance(o, tuple) else [],
            DMA + r[5] * SIZE[DTYPE[r[0]]] * 128 / 220e3, hold=0.06, dma=True)

    sent, lands = [0], []

    def zb(t):
        return R("gz", 2048 + 128 * t, 2176 + 128 * t)

    def send(dst, t, a):
        o, rsem = zb(t), "rz%d" % t
        rid, pid = topo.addr(dst, core)
        m, ne = 0, 0
        for e in topo.engines(core, dst)[:8]:
            m, ne = m | 1 << e, ne + 1
        sent[0] += ne
        k = run("g", [lambda e: e.remote_dma(o[4], a[4], T.sem[rsem], T.sem["snd"], pid, rid, m)], [a], [],
                0.3 if lands else 0.3 + FIRST, sem=("snd", sent[0]))
        src = T.cores[(2 * rank - T.rank_of(dst)) % N]
        n = len(topo.engines(src, core)[:8])
        run("net", [], [], [o], NET, sem=(rsem, n), after=k)
        lands.append((rsem, n))

    dma("y", f("wti"), T.wt[:])
    dma("s", zb(0), T.bites[:, 0:128])
    dma("y", f("bki"), T.bank[:])
    dma("s", f("zb1"), T.bites[:, 128:256])
    dma("y", R("gz", 0, 1024), T.geno[:, 0:1024])
    dma("s", R("gz", 1024, 2048), T.geno[:, 1024:2048])
    dma("y", R("itab", 0, 512), T.immun[:])
    tag[0] = "send1"
    send(T.cores[(rank + 1) % N], 1, f("zb1"))
    tag[0] = "set"

    one, idn, rb = R("onb", 0, 128), R("idw", 16, 144), R("blk", 0, 128, 16)
    row = lambda n, a, b, p=0: R(n, a, b, 1, p, p + 1)
    ms(f("onb"), 1.0)
    keep(f("blk0"), one, [[-16, 8], [0, 16]], O.is_ge, 0.0, 0, 1)
    keep(f("blk"), f("blk0"), [[16, 8], [0, 16]], O.is_ge, 0.0, 15, -1)
    keep(f("hot"), one, [[0, 8], [-1, 16]], O.is_equal, 0.0, 0, 1)
    keep(f("idw"), f("onb"), [[-1, 160]], O.is_equal, 0.0, 16, 1)
    keep(f("iper"), one, [[-32, 4], [-1, 16], [-16, 2]], O.is_equal, 0.0, 0, 1)
    iota(R("kc", 0, 128, 1, 0, 2), [[256, 8], [0, 16]], -PAD - 4096, 0, False)
    iota(row("kc", 0, 128), [[0, 8], [1, 16]], 0, 0, False)
    iota(f("li"), [[16, 8]], 512, 0)
    ms(f("four"), 4.0)
    keep(f("lt4"), f("four"), [[16, 8]], O.is_gt, 0.0, 0, -1)
    ts(f("wlo"), f("wti"), 63, O.bitwise_and)
    ts(f("whi"), f("wti"), 4032, O.bitwise_and)
    cp(f("wlof"), f("wlo"))
    cp(f("whif"), f("whi"))
    act(f("wlb"), f("blk"), scale=f("wlof"))
    ts(f("whb"), f("blk"), f("whif"), O.mult)
    act(f("hotb"), f("hot"), scale=-4194304.0)
    for n, a, b in (("rs", 1.0, 0.0), ("r1", -1e9, 1.0)):
        ms(f(n), a)
        ms(R(n, 0, 128, 16), b)
    for n, c in (("ld", -4096.0), ("lc", 1.0)):
        ms(f(n), 0.0)
        ts(R(n, 15, 143, 16), rb, c, O.mult)
    mm([(R("px", 0, 128), f("hot"), f("hot"), True, True)])
    act(f("m16"), R("px", 0, 16))
    for j in (0, 128):
        act(R("oht", j, j + 128), R("px", 0, 128))
    for a, w in ((256, 256), (512, 256), (768, 256), (2048, PAD - 2048), (1024, 1024)):
        dma("y", R("oht", a, a + w), R("oht", 0, w))
    ms(R("oht", PAD, XW), 0.0)
    ts(f("bt0"), f("bki"), 2047, O.bitwise_and)
    ts(R("btab", 0, 512), f("bt0"), 4097.0 / 4096.0, O.mult)
    ts(f("qr"), f("bki"), -1023.5, O.add, 1.0 / 2048, O.mult)
    act(f("qm"), f("qr"), AF.Identity, bias=12582912.0)
    act(R("qtab", 0, 512), f("qm"), AF.Identity, bias=-12582912.0)
    ms(f("onn"), -0.5)
    act(f("nid"), idn, scale=-1.0)
    act(f("nid2"), idn, scale=-2.0)
    act(f("i2k"), idn, scale=2048.0)
    mm([(R("px", 128, 256), f("blk"), f("iper"), True, True)])
    act(f("nbp"), R("px", 128, 256), scale=-1.0)
    red(f("even"), R("blk", 0, 128, 32))
    red(f("odd"), R("blk", 16, 128, 32))
    ts(f("e16"), f("even"), 16.0, O.mult)
    ts(f("o16"), f("odd"), 16.0, O.mult)
    act(f("ie"), f("idw"), scale=f("e16"))
    act(f("io"), f("idw"), scale=f("o16"))
    turnto = ((R("ie", 16, 144), R("ie", 0, 128)), (R("io", 32, 160), R("io", 16, 144)))
    ms(f("onf"), 1.0)
    scan(f("iv"), f("onf"), f("onf"), O.mult, O.add, -1.0)
    for t in range(5):
        act(R("newr", 128 * t, 128 * t + 128), R("iv", 0, 128), AF.Copy, scale=1.0 + 16 / 4096.0, bias=2048.0 + 128 * t + t / 4096.0)

    def column(n, j, a):
        tt(f("h%d" % j), f("m16"), a, O.mult)
        red(f(n), f("h%d" % j))

    column("rr", 1, R("iv", 0, 16))
    ts(f("r16"), f("rr"), 16.0, O.mult, float(PAD), O.add)
    ts(f("trc"), f("li"), f("rr"), O.add)
    ms(f("half"), 0.5)
    ms(f("zero"), 0.0)
    scan(f("pw"), f("half"), f("zero"), O.mult, O.add, 1024.0)
    for j in (0, 8):
        cp(R("h0", j, j + 8), R("pw", 0, 8))
    column("b6", 2, f("h0"))
    ts(f("uv2"), f("iv"), f("b6"), O.mult)
    ts(f("uv2b"), f("uv2"), 512, O.bitwise_and)
    ts(f("ubt"), f("uv2b"), 1.0 / 512, O.mult)
    red(f("b5"), R("m16", 0, 8))
    act(f("c2"), f("b5"), scale=2.0)
    act(f("c8"), R("m16", 8, 9), scale=2.0, bias=-1.0)
    act(R("ft", 0, 256), f("ubt"), AF.Identity, scale=f("c2"), bias=-1.0)
    act(R("ft", 256, 512), f("ubt"), AF.Identity, scale=f("c2"), bias=f("c8"))
    column("pr", 3, f("pw"))
    ts(f("thr"), f("pr"), 2.5, O.mult)
    ts(f("wc0"), rb, f("pr"), O.mult)
    ts(f("lt4"), f("lt4"), 512.0, O.mult)
    tt(f("wc"), f("wc0"), f("lt4"), O.add)
    for j in range(3):
        ms(row("ordr", 8 * j, 8 * j + 8), 4096.0 * j)
    if OPT["x3s"]:
        ms(row("sev", 0, 32), 0.0)
        ms(row("sev", 32, 48), 7.0)
    for t in range(2):
        step[0] = t
        ms(R("y", 0, 128, 64), 0.0)
        ms(R("x", 2048, XW), 0.0)
        ms(R("x", PAD, XW, 16), -128.0)
        ms(R("Z", 0, 8), PAD + 1)

    def prep(t):
        step[0] = t
        tag[0] = "u"
        z, U = zb(t), R("pu", 0, 128)
        top16 = lambda n: R(n, 0, 128, 1, 0, 16)
        mm(sums(U, [(top16("hot"), top16("hotb")), (f("whb"), z), (f("wlb"), z)]))
        scan(f("us"), f("rs"), U, O.mult, O.min)
        cp(f("ui"), R("us", 15, 128, 16))
        ts(f("ua"), f("ui"), 4095, O.bitwise_and)
        ts(f("xq"), f("ua"), 592.0, O.add)
        tt(f("sq"), f("xq"), f("xq"), O.mult)
        ts(R("bu", 0, 8), f("sq"), 5, O.arith_shift_right, 511, O.bitwise_and)
        tag[0] = "zx"
        zs, zv = OPT["z0"] if t == 0 else OPT["z1"]
        for k in range(16):
            (act if k < zs else cp if k < zs + zv else gcopy)(R("zx", k, 2048, 16), z)
        tag[0] = "dup"
        if t < 3:
            ts(R("bu", 8, 16), f("ui"), 255, O.bitwise_and)
            cp(f("bl"), f("bu"))
            act(R("ub", 0, 128), f("ubt", R("bl", 8, 16)))
            if OPT["crv"]:
                act(R("ub", 128, 256), R("ub", 0, 128), scale=-1.0, bias=1.0)
        else:
            cp(R("bl", 0, 8), R("bu", 0, 8))
        act(f("fe"), f("ft", R("bl", 0, 8)), scale=f("even"))
        act(f("fo"), f("ft", R("bl", 0, 8)), scale=f("odd"))
        for a in range(4):
            ps, l = ("d0", "d1")[a & 1], []
            for j, fx in enumerate(("fe", "fo")):
                x = R(fx, 0, 128, 1, 32 * a, 32 * a + 32)
                l.append((C(ps, 0, 8, 16 * j, 16 * j + 16), x, x, True, True))
            mm(l)
            act(C("e1", 0, 8, 32 * a, 32 * a + 32), C(ps, 0, 8, 0, 32), AF.Relu, bias=-15.0)
        mm([(R("pu", 128 + c, 129 + c), C("e1", c, None, 0, 128), R("wc", c, c + 1), True, True) for c in range(8)])
        ts(f("du"), R("pu", 128, 136), f("thr"), O.is_ge, 1024.0, O.mult)
        tt(f("dtr"), f("du"), f("trc"), O.min)

    KEY = [R("k0", 0, 64), R("k1", 0, 64)]
    half = lambda n, h: R(n, 64 * h, 64 * h + 64)
    A = R("pu", 384, 385)

    def front(t):
        step[0] = t
        tag[0] = "host"
        z = zb(t)
        if t == 0:
            ts(f("vt"), R("bu", 0, 8), 312.0, O.add)
        else:
            ts(f("vt"), R("bu", 0, 8), A, O.add, 1336.0, O.add)
        ts(f("vi"), f("vt"), 511, O.bitwise_and)
        cp(f("vl"), f("vi"))
        tag[0] = "bo"
        cp(f("bo"), R("btab", 0, 512, off=f("vl")))
        act(f("bg"), R("btab", 0, 512, off=f("vl")))
        const = lambda h: (R("onb", 0, 128, 1, 0, 2), R("kc", 64 * h, 64 * h + 64, 1, 0, 2))
        for h in (0, 1):
            mm([(KEY[h],) + const(h) + (True, False)], grp="key%d%d" % (t, h))
        tag[0] = "chunk"
        for a, b in CHUNKS:
            x = R("x", 256 * a, 256 * b)
            tt(x, R("gz", 0, 2048 + 128 * t, off=R("bo", 16 * a, 16 * b)), R("zx", 256 * a, 256 * b), O.subtract)
            act(C("ab", a, b, 0, 256), x, AF.Abs)
            if b in (4, 8):
                h = b // 4 - 1
                mm([(KEY[h], R("ld", 15 - r, 143 - r), C("ab", 4 * h, 4 * h + 4, 16 * r, 16 * r + 16), False, False) for r in range(16)],
                   grp="key%d%d" % (t, h))
        tag[0] = "st"
        gcopy(R("gz", t, 2048, 16), z)
        act(f("qg"), R("qtab", 0, 512, off=f("vl")))
        act(f("pq"), f("qg"), AF.Relu, bias=32.0 * (t + 1), scale=-32.0)
        mm([(C("d0", 8, 12, 16 * h, 16 * h + 16), f("iper"), half("qg", h), True, True) for h in (0, 1)])
        act(f("qp"), C("d0", 8, 12, 0, 32))
        turn(f("tq"), f("qp"))
        W = lambda h: R("pu", 256 + 64 * h, 320 + 64 * h)
        mm([m for h in (0, 1) for m in sums(W(h), [const(h)] + [(turnto[h][j], R("tq", j, 128, 2)) for j in (0, 1)])])
        scan(f("sw"), f("rs"), R("pu", 256, 384), O.mult, O.min)
        ts(f("G0"), R("sw", 15, 128, 16), f("r16"), O.add, 4096.0, O.add)
        tag[0] = "sick"
        if OPT["sick"] == 0:
            act(f("ig"), R("itab", 0, 512, off=f("vl")))
            mm(sums(R("pi", 0, 128), [(idn, z), (f("nid"), f("ig"))]))
            act(f("gs"), R("pi", 0, 128), AF.Sign, bias=-0.5)
            if OPT["immv"]:
                act(f("im1"), R("pi", 0, 128), scale=-1.0, bias=-1.0)
            else:
                act(f("im1"), f("ig"), bias=-1.0)
        else:
            tt(f("ig"), R("itab", 0, 512, off=f("vl")), z, O.subtract)
            act(f("gs"), f("ig"), AF.Sign, bias=-0.5, scale=-1.0)
            act(f("im1"), f("ig"), bias=-1.0)
        mm([m for h in (0, 1) for m in sums(C("d1", 8, 12, 16 * h, 16 * h + 16), [(f("iper"), half("pq", h)), (f("nbp"), half("gs", h))])])
        act(f("pen"), C("d1", 8, 12, 0, 32), AF.Relu, bias=524288.0, scale=524288.0)
        turn(f("tp"), f("pen"))
        for h in (0, 1):
            tag[0] = "sick"
            mm([(KEY[h], turnto[h][j], R("tp", j, 128, 2), False, j == 1) for j in (0, 1)], grp="key%d%d" % (t, h))
            tag[0] = "top"
            a = 64 * h
            scan(R("ss", a, a + 64), R("r1", 0, 64), KEY[h], O.max, O.min)
            tt(R("y", a + 1, a + 64), R("ss", a, a + 63), R("k%d" % h, 1, 64), O.max)
            scan(R("ss", 128 + a, 192 + a), R("y", a, a + 64), R("rs", 0, 64), O.min, O.mult)
        tag[0] = "awake"
        if t < 4:
            act(f("sg"), R("ss", 15, 256, 16), AF.Sign, bias=0.5, accum_out=f("ac"))
            mm([(A, f("onn"), f("ac"), True, True)])
        tag[0] = "rows"
        ts(f("mi"), R("ss", 15, 256, 16), f("r16"), O.add)
        ts(R("Z", 8, 24), f("mi"), 4095, O.bitwise_and)
        cp(R("xl", 0, 16), R("Z", 8, 24))
        tt(f("Zm"), R("Z", 8, 16), R("Z", 16, 24), O.min)
        tt(R("Z", 24, 32), f("Zm"), f("G0"), O.min)
        tt(R("Z", 32, 40), f("vi"), f("dtr"), O.max)
        cp(R("xl", 16, 32), R("Z", 24, 40))
        tt(f("nv"), f("oht", R("xl", 16, 24)), R("newr", 128 * t, 128 * t + 128), O.mult)
        tt(R("btab", 0, 640, off=R("xl", 24, 32)), f("bg"), f("nv"), O.max)

    def back(t):
        step[0] = t
        tag[0] = "stw"
        z, ol = zb(t), R("xl", 24, 32)
        blk3 = lambda n, j, l=1: R(n, 128 * j, 128 * (j + l))
        act(f("za"), f("oht", R("xl", 0, 24)), scale=8.0 + t)
        QP = R("pi", 128, 256)
        if OPT["qs"]:
            mm(sums(QP, [(idn, f("qg"))] + [(f("nid2"), blk3("za", j)) for j in range(3)]))
            act(f("qn"), QP, AF.Relu)
            tt(R("qtab", 0, 640, off=ol), f("qn"), blk3("za", 2), O.add)
        else:
            mm(sums(QP, [(idn, f("qg"))] + [(f("nid2"), blk3("za", j)) for j in range(2)]))
            tt(f("qn"), QP, blk3("za", 2), O.max)
            cp(R("qtab", 0, 640, off=ol), f("qn"))
        tag[0] = "post"
        act(blk3("X", 0, 2), f("x", R("xl", 0, 16)))
        ts(blk3("cm", 0), blk3("X", 0), 0.0, O.is_gt)
        ts(blk3("cm", 1, 2), blk3("X", 0, 2), 0.0, O.is_lt)
        CN = R("pc", 128, 176)
        cnt = [(R("lc", 15 - r, 143 - r), R("cm", r, 768, 16)) for r in range(16)]
        if OPT["x3s"]:
            ts(blk3("cm", 3), blk3("X", 1), 0.0, O.is_gt)
            mm(sums(R("pc", 0, 128), [(idn, blk3("X", 1)), (f("nid"), blk3("X", 0))]))
            act(blk3("cm", 4), R("pc", 0, 128), AF.Sign, bias=-0.5)
            act(blk3("cm", 5), R("pc", 0, 128), AF.Sign, bias=-0.5, scale=-1.0)
            cnt = [(row("onb", 0, 128), row("sev", 0, 48))] + cnt
        else:
            tt(blk3("X", 2), blk3("X", 1), blk3("X", 0), O.subtract)
            ts(blk3("cm", 3, 2), blk3("X", 1, 2), 0.0, O.is_gt)
            ts(blk3("cm", 5), blk3("X", 2), 0.0, O.is_lt)
        mm(sums(CN, cnt))
        ts(f("bb"), CN, 9.0, O.is_ge, 16384.0, O.mult)
        P = R("pc", 192, 216)
        mm(sums(P, [(row("onb", 0, 128), row("ordr", 0, 24)), (idn, R("bb", 0, 24)), (idn, R("bb", 24, 48))]))
        tt(f("K"), P, R("Z", 0, 24), O.add)
        K = lambda j: R("K", 8 * j, 8 * j + 8)
        m = lambda j: R("mm", 8 * j, 8 * j + 8)
        tt(m(0), K(0), K(1), O.min)
        tt(m(1), K(0), K(1), O.max)
        tt(m(2), m(1), K(2), O.min)
        tt(R("fm", 0, 8), m(0), K(2), O.min)
        w = 16 if t < 3 else 8
        if t < 3:
            tt(R("fm", 8, 16), m(0), m(2), O.max)
        else:
            ops.pop(-2), ops.pop(-2)
        ts(R("fa", 0, w), R("fm", 0, w), 4095, O.bitwise_and)
        cp(R("fl", 0, w), R("fa", 0, w))
        if not (OPT["immv"] and (t > 2 or OPT["crv"])):
            act(R("xf", 0, 16 * w), f("x", R("fl", 0, w)))
        tag[0] = "cross"
        if t < 3:
            d, c = R("px", 0, 128), R("px", 128, 256)
            if OPT["crv"]:
                tt(f("db"), f("x", f("fl")), f("ub"), O.mult)
                mm(sums(c, [(idn, z), (idn, blk3("db", 0)), (idn, blk3("db", 1))]))
            else:
                mm(sums(d, [(idn, blk3("xf", 0)), (f("nid"), blk3("xf", 1))]))
                tt(blk3("db", 0), d, blk3("ub", 0), O.mult)
                mm(sums(c, [(idn, z), (idn, blk3("xf", 1)), (idn, blk3("db", 0))]))
            act(f("cr%d" % t), c)
            send(T.cores[(rank + 2) % N], t + 2, f("cr%d" % t))
        tag[0] = "imm"
        if OPT["immv"]:
            tt(f("inn"), f("x", R("fl", 0, 8)), f("im1"), O.max)
            tt(R("itab", 0, 640, off=ol), f("inn"), z, O.add)
        else:
            FP = R("pi", 256, 384)
            mm(sums(FP, [(idn, z), (idn, blk3("xf", 0))]))
            tt(f("inn"), FP, f("im1"), O.max)
            cp(R("itab", 0, 640, off=ol), f("inn"))

    prep(0)
    for t in range(5):
        front(t)
        if t < 4:
            prep(t + 1)
        back(t)
    tag[0] = "end"
    dma("y", T.ygeno[:], R("gz", 0, 2048))
    for j in (0, 1):
        a, b = 256 * j, 256 * j + 256
        ts(R("bki", a, b), R("btab", a, b), 4096.0, O.mult)
        ts(R("bt0", a, b), R("bki", a, b), 4095, O.bitwise_and)
        mm([(R("k%d" % j, 0, 256), f("i2k"), R("qtab", a, b), True, True)])
        tt(R("yb", a, b), R("k%d" % j, 0, 256), R("bt0", a, b), O.add)
        dma("y", T.ybank[:, a:b], R("yb", a, b))
    dma("s", T.yimm[:], R("itab", 0, 512))

    def clash(r, w, r2, w2):
        return (w or w2) and r[1] & r2[1] and r[2] < r2[3] and r2[2] < r[3]

    pred, seen = [], {}
    for k, o in enumerate(ops):
        p = {o["after"]} if "after" in o else set()
        for r, w in o["regs"]:
            for k2, r2, w2 in seen.get(r[0], ()):
                if k2 not in p and clash(r, w, r2, w2):
                    p.add(k2)
        for r, w in o["regs"]:
            seen.setdefault(r[0], []).append((k, r, w))
        pred.append(p)
    succ = [[] for _ in ops]
    for k, p in enumerate(pred):
        for k2 in p:
            succ[k2].append(k)
    way = [0.0] * len(ops)
    for k in range(len(ops) - 1, -1, -1):
        way[k] = ops[k]["cost"] + max([WAKE + way[j] for j in succ[k]] + [0.0])
    way = [w + BONUS.get(o["tag"], 0.0) for w, o in zip(way, ops)]
    left = [len(p) for p in pred]
    ready = [k for k in range(len(ops)) if not left[k]]
    end, free, bank, order = [0.0] * len(ops), {}, {}, []
    while ready:
        best, at = {}, {}
        for k in ready:
            o = ops[k]
            q = o["q"]
            s = free.get(q, 0.0)
            for j in pred[k]:
                s = max(s, end[j] + WAKE)
            for r, w in o["regs"]:
                for q2, e in bank.get(r[0], {}).items():
                    if q2 != q:
                        s = max(s, e + WAKE)
            at[k] = s
            best[q] = min(best.get(q, 1e9), s + o.get("hold", o["cost"]))
        q = min((at[k], ops[k]["q"]) for k in ready)[1]
        k = -max((way[k], -k) for k in ready if ops[k]["q"] == q and at[k] < best[q])[1]
        o = ops[k]
        ready.remove(k)
        order.append(k)
        end[k] = at[k] + o["cost"]
        if q != "net":
            free[q] = at[k] + o.get("hold", o["cost"])
        for r, w in o["regs"]:
            if r[0] in PS:
                bank.setdefault(r[0], {})[q] = end[k]
        for j in succ[k]:
            left[j] -= 1
            if not left[j]:
                ready.append(j)

    know = {q: 0 for q in eng}
    place = {k: n for n, k in enumerate(order)}
    done, semof, acc, chains, used = {}, {}, {}, [], {"c": 0, "d": 0}
    for k in order:
        o = ops[k]
        q, grp = o["q"], o.get("grp")
        if q == "net":
            done[k], semof[k] = 1 << k, o["sem"]
        else:
            need = set()
            for r, w in o["regs"]:
                for k2, q2, r2, w2, g2 in acc.get(r[0], ()):
                    if know[q] >> k2 & 1 or (grp is not None and g2 == grp):
                        continue
                    if (r[0] in PS and q2 != q) or clash(r, w, r2, w2):
                        need.add((-place[k2], k2))
            for _, k2 in sorted(need):
                if not know[q] >> k2 & 1:
                    eng[q].wait_ge(T.sem[semof[k2][0]], semof[k2][1])
                    know[q] |= done[k2]
            done[k] = know[q] | 1 << k
            if o.get("dma"):
                nm = "d%d" % used["d"]
                used["d"] += 1
                semof[k] = (nm, 16)
                chains.append([nm, 16, k, False])
                o["calls"][0](eng[q]).then_inc(T.sem[nm], 16)
            elif "sem" in o:
                semof[k] = o["sem"]
                o["calls"][0](eng[q])
            else:
                ch = None
                for c in chains:
                    if c[3] and know[q] >> c[2] & 1:
                        ch = c
                        break
                if ch is None:
                    ch = ["c%d" % used["c"], 0, k, True]
                    used["c"] += 1
                    chains.append(ch)
                ch[1] += len(o["calls"])
                ch[2] = k
                semof[k] = (ch[0], ch[1])
                for c in o["calls"]:
                    c(eng[q]).then_inc(T.sem[ch[0]], 1)
        for r, w in o["regs"]:
            acc.setdefault(r[0], []).append((k, q, r, w, grp))
    for nm, n, _, _ in chains:
        g.wait_ge(T.sem[nm], n)
    for nm, n in lands:
        g.wait_ge(T.sem[nm], n)
    g.wait_ge(T.sem["snd"], sent[0])
